import numpy as np
import ml_dtypes


def mxq(x, axis, fmt="e4m3"):
    dtype, down = {"e4m3": (ml_dtypes.float8_e4m3fn, 7), "e5m2": (ml_dtypes.float8_e5m2, 14)}[fmt]
    v = np.moveaxis(np.asarray(x, np.float32).astype(ml_dtypes.bfloat16).astype(np.float64), axis, -1)
    blocks = v.reshape(v.shape[:-1] + (-1, 32))
    amax = np.abs(blocks).max(-1, keepdims=True)
    byte = np.maximum(np.where(amax > 0, np.frexp(amax)[1] - 1 + 127, 0) - down, 1)
    scale = np.exp2(byte - 127.0)
    codes = (blocks / scale).astype(np.float32).astype(dtype).astype(np.float64)
    return np.moveaxis((codes * scale).reshape(v.shape), -1, axis)


WIDE = False


def mx_kscale(k):
    if not WIDE:
        return np.ones(k)
    levels = np.array([10, -10, 5, -5, 0])
    if k % 512:
        return np.exp2(np.random.permutation(np.resize(levels, k // 32))).repeat(32)
    a = np.empty((k // 512, 16))
    for p in range(k // 512):
        a[p, :8] = np.random.permutation(np.resize(levels, 8))
        for g in range(8):
            far = levels[np.abs(levels - a[p, g]) >= 10]
            a[p, g + 8] = far[np.random.randint(len(far))]
    return np.exp2(a.ravel()).repeat(32)


def f64(x):
    return np.asarray(x).astype(np.float64)


def striped(idx):
    return np.tile(idx.reshape(-1, 16).T, (8, 1)).astype(np.uint16)


def unstriped(offs):
    return offs[:16].T.reshape(-1).astype(np.int64)


def pack_weight(w):
    k, n = w.shape
    w = f64(np.asarray(w, np.float32).astype(ml_dtypes.bfloat16)).reshape(k // 32, 32, n)
    amax = np.abs(w).max(1)
    byte = np.clip(np.where(amax > 0, np.frexp(amax)[1] - 1 + 127 - 7, 1), 1, 254)
    scaled = (w * np.exp2(127.0 - byte)[:, None, :]).reshape(k, n).astype(np.float32)
    words = np.ascontiguousarray(scaled.reshape(k // 512, 128, 4, n).transpose(0, 1, 3, 2)).astype(ml_dtypes.float8_e4m3fn).view(np.uint8)
    return words, np.ascontiguousarray(byte.astype(np.uint8).reshape(k // 512, 16, n))


def unpack_weight(words, scales):
    g, p, n, _ = words.shape
    vals = np.ascontiguousarray(words).view(ml_dtypes.float8_e4m3fn).astype(np.float64) * np.repeat(np.exp2(scales.astype(np.float64) - 127.0), 8, axis=1)[..., None]
    return vals.transpose(0, 1, 3, 2).reshape(g * 512, n)


def relu(v):
    return np.maximum(v, 0.0)


K, T, D, S, V, N = 1536, 512, 4, 1024, 256, 256


def setup_inputs():
    n = np.random.standard_normal
    s = mx_kscale(K)[:, None]
    words, scales = pack_weight(n((K, N)) / np.sqrt(K) / s)
    return {
        "xT": (n((K, T)) * s).astype(np.float32),
        "w_words": words,
        "w_scales": scales,
        "b": (0.3 * n((N, 1))).astype(np.float32),
        "gate": np.tile(np.random.uniform(0.2, 1.0, (D, 1, V)) / np.sqrt(D), (1, N, 1)).astype(np.float32),
        "pos1": striped(np.random.permutation(T)[:V]),
        "pos2": striped(np.random.permutation(T)[:V]),
        "pos3": striped(np.random.permutation(T)[:V]),
        "pos4": striped(np.random.permutation(T)[:V]),
    }


def reference(xT, w_words, w_scales, b, gate, pos1, pos2, pos3, pos4):
    w = unpack_weight(w_words, w_scales)
    y = w.T @ mxq(f64(xT), 0, "e4m3")
    y = relu(y + f64(b))
    return sum(f64(gate[d]) * y[:, unstriped(p)] for d, p in enumerate((pos1, pos2, pos3, pos4)))

@@ -1,0 +1,178 @@
+from contextlib import ExitStack
+
+import concourse.mybir as mybir
+from concourse.masks import make_identity
+
+K, T, D, V, N = 1536, 512, 4, 256, 256
+FLOPS = 2 * K * T * N
+
+F32 = mybir.dt.float32
+BF16 = mybir.dt.bfloat16
+I32 = mybir.dt.int32
+U32 = mybir.dt.uint32
+U16 = mybir.dt.uint16
+U8 = mybir.dt.uint8
+FP8X4 = mybir.dt.float8_e4m3fn_x4
+RELU = mybir.ActivationFunctionType.Relu
+ADD, MULT, MAX = mybir.AluOpType.add, mybir.AluOpType.mult, mybir.AluOpType.max
+
+P = 128
+PACK = 4
+PASSES = K // (P * PACK)
+BLOCKS = N // P
+
+CHUNKS = ((0, 0, 512), (1, 0, 512), (2, 0, 384), (2, 384, 128))
+GROUPS = ((0, 128), (128, 256), (384, 128))
+
+
+def tile_picked_agg_lin_relu_sub_l_kernel(tc, xT, w_words, w_scales, b, gate, pos1, pos2, pos3, pos4, out):
+    nc = tc.nc
+    with ExitStack() as ctx:
+        keep = ctx.enter_context(tc.tile_pool(name="keep", bufs=1))
+        psum = ctx.enter_context(tc.psum_pool(name="psum", bufs=1))
+
+        lists = [keep.tile([P, V // 16], U16, name=f"list{d}") for d in range(D)]
+        raw = [keep.tile([P, PACK, n], F32, name=f"raw{i}") for i, (a, t0, n) in enumerate(CHUNKS)]
+        grouped = [keep.tile([P, n, PACK], BF16, align_bytes=64, name=f"grouped{i}") for i, (a, t0, n) in enumerate(CHUNKS)]
+        codes = [keep.tile([P, n], U32, align_bytes=64, name=f"codes{i}") for i, (a, t0, n) in enumerate(CHUNKS)]
+        scales = [keep.tile([P, n], U8, align_bytes=64, name=f"scales{i}") for i, (a, t0, n) in enumerate(CHUNKS)]
+        w_sb = [keep.tile([P, PASSES, P * PACK], U8, align_bytes=64, name=f"w_sb{m}") for m in range(BLOCKS)]
+        w_sc = keep.tile([P, PASSES, N], U8, align_bytes=64, name="w_sc")
+        bias = keep.tile([P, BLOCKS], F32, name="bias")
+        identity = keep.tile([P, P], F32, name="identity")
+        bias_rows = keep.tile([P, P], F32, name="bias_rows")
+        bias_psum = psum.tile([P, P], F32, name="bias_psum")
+        gates = [keep.tile([P, D, V], F32, name=f"gates{m}") for m in range(BLOCKS)]
+        y = [keep.tile([P, T], F32, name=f"y{m}") for m in range(BLOCKS)]
+        picked = [keep.tile([P, D, V], F32, name=f"picked{m}") for m in range(BLOCKS)]
+        half = [keep.tile([P, 2, V], F32, name=f"half{m}") for m in range(BLOCKS)]
+        result = [keep.tile([P, V], F32, name=f"result{m}") for m in range(BLOCKS)]
+        warm = keep.tile([P, 8], F32, name="warm")
+        acc = [[psum.tile([P, n], F32, name=f"acc{m}_{g}") for g, (t0, n) in enumerate(GROUPS)] for m in range(BLOCKS)]
+
+        x_rows = xT.rearrange("(a p j) t -> a p j t", p=P, j=PACK)
+
+        def load(i):
+            a, t0, n = CHUNKS[i]
+            nc.sync.dma_start(out=raw[i][:], in_=x_rows[a][:, :, t0 : t0 + n])
+
+        def interleave(copy, i, c0, c1):
+            copy(
+                out=grouped[i][:, c0:c1, :].rearrange("p (c i) j -> p c j i", i=4),
+                in_=raw[i][:, :, c0:c1].rearrange("p j (c i) -> p c j i", i=4),
+            )
+
+        def quantize(i, c0, c1):
+            nc.vector.quantize_mx(
+                out=codes[i][:, c0:c1].bitcast(FP8X4),
+                scales=scales[i][:, c0:c1],
+                in_=grouped[i][:, c0:c1, :].rearrange("p c j -> p (c j)"),
+            )
+
+        def multiply(i, g, m):
+            a, c0, cn = CHUNKS[i]
+            t0, n = GROUPS[g]
+            s = slice(t0 - c0, t0 - c0 + n)
+            nc.tensor.matmul_mx(
+                out=acc[m][g][:],
+                lhsT=w_sb[m][:, a, :].bitcast(FP8X4),
+                lhsT_scale=w_sc[:, a, m * P : (m + 1) * P],
+                rhs=codes[i][:, s].bitcast(FP8X4),
+                rhs_scale=scales[i][:, s],
+                start=(a == 0),
+                stop=(a == PASSES - 1),
+            )
+
+        def finish_scalar(g, m):
+            t0, n = GROUPS[g]
+            nc.scalar.activation(out=y[m][:, t0 : t0 + n], in_=acc[m][g][:], func=RELU, bias=bias[:, m : m + 1], scale=1.0)
+
+        def finish_vector(g, m):
+            t0, n = GROUPS[g]
+            nc.vector.tensor_scalar(out=y[m][:, t0 : t0 + n], in0=acc[m][g][:], scalar1=bias[:, m : m + 1], scalar2=0.0, op0=ADD, op1=MAX)
+
+        def gather(m, d):
+            nc.vector.tensor_tensor(picked[m][:, d, :], y[m][:].indirect(lists[d][:]), gates[m][:, d, :], MULT)
+
+        def store(m, v0=0, v1=V):
+            nc.sync.dma_start(out=out[m * P : (m + 1) * P, v0:v1], in_=result[m][:, v0:v1])
+
+        nc.vector.memset(w_sc[:].rearrange("p a n -> p (a n)").bitcast(I32), 0)
+        nc.vector.memset(warm[:], 0.0)
+
+        def load_w(m, a0, a1):
+            nc.sync.dma_start(out=w_sb[m][:, a0:a1, :], in_=w_words[a0:a1, :, m * P : (m + 1) * P, :].rearrange("a p n r -> p a (n r)"))
+
+        def load_gate(m, d0, d1):
+            nc.sync.dma_start(out=gates[m][:, d0:d1, :], in_=gate[d0:d1, m * P : (m + 1) * P, :].rearrange("d p v -> p d v"))
+
+        def load_list(d):
+            nc.sync.dma_start(lists[d][:], (pos1, pos2, pos3, pos4)[d])
+
+        make_identity(nc, identity[:])
+        nc.vector.memset(bias_rows[:], 0.0)
+        nc.scalar.dma_start(out=bias_rows[0:BLOCKS, :], in_=b.rearrange("(m p) o -> m (p o)", p=P))
+        load(0)
+        for q in range(4):
+            nc.sync.dma_start(
+                out=w_sc[32 * q : 32 * q + 4, :, :].bitcast(I32),
+                in_=w_scales[:, 4 * q : 4 * q + 4, :].rearrange("a r n -> r a n").bitcast(I32),
+            )
+        load(1)
+        load_w(0, 0, 2)
+        for i in range(2, len(CHUNKS)):
+            load(i)
+        load_w(0, 2, 3)
+        load_list(0)
+        load_list(1)
+        load_gate(0, 0, 2)
+        load_w(1, 0, 3)
+        load_list(2)
+        load_gate(0, 2, 4)
+        load_list(3)
+        load_gate(1, 0, 2)
+        load_gate(1, 2, 4)
+        nc.tensor.transpose(bias_psum[:], bias_rows[:], identity[:])
+        nc.vector.tensor_copy(out=bias[:], in_=bias_psum[:, 0:BLOCKS])
+
+        nc.scalar.activation(out=warm[:, 0:1], in_=warm[:, 1:2], func=RELU)
+
+        for i in (0, 1):
+            interleave(nc.vector.tensor_copy, i, 0, 320)
+            interleave(nc.scalar.copy, i, 320, 512)
+            quantize(i, 0, 512)
+            for g in range(3):
+                multiply(i, g, 0)
+        interleave(nc.vector.tensor_copy, 2, 0, 128)
+        interleave(nc.scalar.copy, 2, 256, 384)
+        interleave(nc.vector.tensor_copy, 2, 128, 256)
+        interleave(nc.scalar.copy, 3, 64, 128)
+        quantize(2, 0, 128)
+        multiply(2, 0, 0)
+        interleave(nc.vector.tensor_copy, 3, 0, 64)
+        quantize(2, 128, 384)
+        multiply(2, 1, 0)
+        finish_scalar(0, 0)
+        quantize(3, 0, 128)
+        multiply(3, 2, 0)
+        finish_scalar(1, 0)
+        finish_scalar(2, 0)
+        for g in range(3):
+            for i in (0, 1, 2 if g < 2 else 3):
+                multiply(i, g, 1)
+            finish_scalar(g, 1)
+
+
+        for d in range(D):
+            gather(0, d)
+        gather(1, 0)
+        gather(1, 1)
+        nc.vector.tensor_tensor(half[0][:], picked[0][:, 0:2, :], picked[0][:, 2:4, :], ADD)
+        gather(1, 2)
+        nc.vector.tensor_tensor(half[1][:, 0, :], picked[1][:, 0, :], picked[1][:, 1, :], ADD)
+        gather(1, 3)
+        nc.vector.tensor_tensor(half[1][:, 1, :], half[1][:, 0, :], picked[1][:, 2, :], ADD)
+        nc.vector.tensor_tensor(result[0][:], half[0][:, 0, :], half[0][:, 1, :], ADD)
+        store(0)
+        nc.vector.tensor_tensor(result[1][:], half[1][:, 1, :], picked[1][:, 3, :], ADD)
+        store(1)

@@ -14,7 +14,7 @@ U16 = mybir.dt.uint16
 U8 = mybir.dt.uint8
 FP8X4 = mybir.dt.float8_e4m3fn_x4
 RELU = mybir.ActivationFunctionType.Relu
-ADD, MULT, MAX = mybir.AluOpType.add, mybir.AluOpType.mult, mybir.AluOpType.max
+ADD, MULT = mybir.AluOpType.add, mybir.AluOpType.mult
 
 P = 128
 PACK = 4
@@ -34,21 +34,22 @@ def tile_picked_agg_lin_relu_sub_l_kernel(tc, xT, w_words, w_scales, b, gate, po
         lists = [keep.tile([P, V // 16], U16, name=f"list{d}") for d in range(D)]
         raw = [keep.tile([P, PACK, n], F32, name=f"raw{i}") for i, (a, t0, n) in enumerate(CHUNKS)]
         grouped = [keep.tile([P, n, PACK], BF16, align_bytes=64, name=f"grouped{i}") for i, (a, t0, n) in enumerate(CHUNKS)]
-        codes = [keep.tile([P, n], U32, align_bytes=64, name=f"codes{i}") for i, (a, t0, n) in enumerate(CHUNKS)]
-        scales = [keep.tile([P, n], U8, align_bytes=64, name=f"scales{i}") for i, (a, t0, n) in enumerate(CHUNKS)]
+        codes = [keep.tile([P, T], U32, align_bytes=64, name=f"codes{a}") for a in range(PASSES)]
+        scales = [keep.tile([P, T], U8, align_bytes=64, name=f"scales{a}") for a in range(PASSES)]
         w_sb = [keep.tile([P, PASSES, P * PACK], U8, align_bytes=64, name=f"w_sb{m}") for m in range(BLOCKS)]
         w_sc = keep.tile([P, PASSES, N], U8, align_bytes=64, name="w_sc")
         bias = keep.tile([P, BLOCKS], F32, name="bias")
         identity = keep.tile([P, P], F32, name="identity")
         bias_rows = keep.tile([P, P], F32, name="bias_rows")
-        bias_psum = psum.tile([P, P], F32, name="bias_psum")
-        gates = [keep.tile([P, D, V], F32, name=f"gates{m}") for m in range(BLOCKS)]
+        bias_psum = psum.tile([P, P], F32, name="bias_psum", tag="turned1_1")
+        gates = keep.tile([P, D, V], F32, name="gates")
         y = [keep.tile([P, T], F32, name=f"y{m}") for m in range(BLOCKS)]
         picked = [keep.tile([P, D, V], F32, name=f"picked{m}") for m in range(BLOCKS)]
-        half = [keep.tile([P, 2, V], F32, name=f"half{m}") for m in range(BLOCKS)]
+        turned_sb = [[keep.tile([P, P], F32, name=f"turned_sb{m}_{h}") for h in range(2)] for m in range(BLOCKS)]
         result = [keep.tile([P, V], F32, name=f"result{m}") for m in range(BLOCKS)]
         warm = keep.tile([P, 8], F32, name="warm")
-        acc = [[psum.tile([P, n], F32, name=f"acc{m}_{g}") for g, (t0, n) in enumerate(GROUPS)] for m in range(BLOCKS)]
+        acc = [psum.tile([P, n], F32, name=f"acc0_{g}", tag=f"acc0_{g}") for g, (t0, n) in enumerate(GROUPS)]
+        acc1 = psum.tile([P, T], F32, name="acc1", tag="acc1")
 
         x_rows = xT.rearrange("(a p j) t -> a p j t", p=P, j=PACK)
 
@@ -63,36 +64,35 @@ def tile_picked_agg_lin_relu_sub_l_kernel(tc, xT, w_words, w_scales, b, gate, po
             )
 
         def quantize(i, c0, c1):
+            a, t0, n = CHUNKS[i]
             nc.vector.quantize_mx(
-                out=codes[i][:, c0:c1].bitcast(FP8X4),
-                scales=scales[i][:, c0:c1],
+                out=codes[a][:, t0 + c0 : t0 + c1].bitcast(FP8X4),
+                scales=scales[a][:, t0 + c0 : t0 + c1],
                 in_=grouped[i][:, c0:c1, :].rearrange("p c j -> p (c j)"),
             )
 
-        def multiply(i, g, m):
-            a, c0, cn = CHUNKS[i]
-            t0, n = GROUPS[g]
-            s = slice(t0 - c0, t0 - c0 + n)
+        def multiply(bank, a, t0, n, m):
             nc.tensor.matmul_mx(
-                out=acc[m][g][:],
+                out=bank[:],
                 lhsT=w_sb[m][:, a, :].bitcast(FP8X4),
                 lhsT_scale=w_sc[:, a, m * P : (m + 1) * P],
-                rhs=codes[i][:, s].bitcast(FP8X4),
-                rhs_scale=scales[i][:, s],
+                rhs=codes[a][:, t0 : t0 + n].bitcast(FP8X4),
+                rhs_scale=scales[a][:, t0 : t0 + n],
                 start=(a == 0),
                 stop=(a == PASSES - 1),
             )
 
-        def finish_scalar(g, m):
-            t0, n = GROUPS[g]
-            nc.scalar.activation(out=y[m][:, t0 : t0 + n], in_=acc[m][g][:], func=RELU, bias=bias[:, m : m + 1], scale=1.0)
+        def multiply0(a, g):
+            multiply(acc[g], a, *GROUPS[g], 0)
 
-        def finish_vector(g, m):
-            t0, n = GROUPS[g]
-            nc.vector.tensor_scalar(out=y[m][:, t0 : t0 + n], in0=acc[m][g][:], scalar1=bias[:, m : m + 1], scalar2=0.0, op0=ADD, op1=MAX)
+        def finish(bank, t0, n, m):
+            nc.scalar.activation(out=y[m][:, t0 : t0 + n], in_=bank[:], func=RELU, bias=bias[:, m : m + 1], scale=1.0)
+
+        def product(m, d):
+            return gates[:, 2, :] if (m, d) == (0, 3) else picked[m][:, d, :]
 
         def gather(m, d):
-            nc.vector.tensor_tensor(picked[m][:, d, :], y[m][:].indirect(lists[d][:]), gates[m][:, d, :], MULT)
+            nc.vector.tensor_tensor(product(m, d), y[m][:].indirect(lists[d][:]), gates[:, d, :], MULT)
 
         def store(m, v0=0, v1=V):
             nc.sync.dma_start(out=out[m * P : (m + 1) * P, v0:v1], in_=result[m][:, v0:v1])
@@ -103,8 +103,8 @@ def tile_picked_agg_lin_relu_sub_l_kernel(tc, xT, w_words, w_scales, b, gate, po
         def load_w(m, a0, a1):
             nc.sync.dma_start(out=w_sb[m][:, a0:a1, :], in_=w_words[a0:a1, :, m * P : (m + 1) * P, :].rearrange("a p n r -> p a (n r)"))
 
-        def load_gate(m, d0, d1):
-            nc.sync.dma_start(out=gates[m][:, d0:d1, :], in_=gate[d0:d1, m * P : (m + 1) * P, :].rearrange("d p v -> p d v"))
+        def load_gate(d0, d1):
+            nc.sync.dma_start(out=gates[:, d0:d1, :], in_=gate[d0:d1, 0:P, :].rearrange("d p v -> p d v"))
 
         def load_list(d):
             nc.sync.dma_start(lists[d][:], (pos1, pos2, pos3, pos4)[d])
@@ -125,13 +125,11 @@ def tile_picked_agg_lin_relu_sub_l_kernel(tc, xT, w_words, w_scales, b, gate, po
         load_w(0, 2, 3)
         load_list(0)
         load_list(1)
-        load_gate(0, 0, 2)
+        load_gate(0, 2)
         load_w(1, 0, 3)
         load_list(2)
-        load_gate(0, 2, 4)
+        load_gate(2, 4)
         load_list(3)
-        load_gate(1, 0, 2)
-        load_gate(1, 2, 4)
         nc.tensor.transpose(bias_psum[:], bias_rows[:], identity[:])
         nc.vector.tensor_copy(out=bias[:], in_=bias_psum[:, 0:BLOCKS])
 
@@ -142,37 +140,38 @@ def tile_picked_agg_lin_relu_sub_l_kernel(tc, xT, w_words, w_scales, b, gate, po
             interleave(nc.scalar.copy, i, 320, 512)
             quantize(i, 0, 512)
             for g in range(3):
-                multiply(i, g, 0)
+                multiply0(i, g)
         interleave(nc.vector.tensor_copy, 2, 0, 128)
         interleave(nc.scalar.copy, 2, 256, 384)
         interleave(nc.vector.tensor_copy, 2, 128, 256)
         interleave(nc.scalar.copy, 3, 64, 128)
         quantize(2, 0, 128)
-        multiply(2, 0, 0)
+        multiply0(2, 0)
         interleave(nc.vector.tensor_copy, 3, 0, 64)
         quantize(2, 128, 384)
-        multiply(2, 1, 0)
-        finish_scalar(0, 0)
+        multiply0(2, 1)
+        finish(acc[0], *GROUPS[0], 0)
         quantize(3, 0, 128)
-        multiply(3, 2, 0)
-        finish_scalar(1, 0)
-        finish_scalar(2, 0)
-        for g in range(3):
-            for i in (0, 1, 2 if g < 2 else 3):
-                multiply(i, g, 1)
-            finish_scalar(g, 1)
+        multiply0(2, 2)
+        finish(acc[1], *GROUPS[1], 0)
+        finish(acc[2], *GROUPS[2], 0)
+        for a in range(PASSES):
+            multiply(acc1, a, 0, T, 1)
+        finish(acc1, 0, T, 1)
 
-
-        for d in range(D):
-            gather(0, d)
-        gather(1, 0)
-        gather(1, 1)
-        nc.vector.tensor_tensor(half[0][:], picked[0][:, 0:2, :], picked[0][:, 2:4, :], ADD)
-        gather(1, 2)
-        nc.vector.tensor_tensor(half[1][:, 0, :], picked[1][:, 0, :], picked[1][:, 1, :], ADD)
-        gather(1, 3)
-        nc.vector.tensor_tensor(half[1][:, 1, :], half[1][:, 0, :], picked[1][:, 2, :], ADD)
-        nc.vector.tensor_tensor(result[0][:], half[0][:, 0, :], half[0][:, 1, :], ADD)
-        store(0)
-        nc.vector.tensor_tensor(result[1][:], half[1][:, 1, :], picked[1][:, 3, :], ADD)
-        store(1)
+        back = []
+        for m in range(BLOCKS):
+            turned = [psum.tile([P, P], F32, name=f"turned{m}_{h}", tag=f"turned{m}_{h}") for h in range(2)]
+            for d in range(D - 1):
+                gather(m, d)
+                for h in range(2):
+                    nc.tensor.matmul(turned[h][:], lhsT=picked[m][:, d, h * P : (h + 1) * P], rhs=identity[:], is_transpose=True, start=(d == 0), stop=(d == D - 2))
+            back.append(psum.tile([P, V], F32, name=f"back{m}", tag=f"acc0_{m}"))
+            for h in range(2):
+                nc.scalar.copy(out=turned_sb[m][h][:], in_=turned[h][:])
+                nc.tensor.transpose(back[m][:, h * P : (h + 1) * P], turned_sb[m][h][:], identity[:])
+        for m in range(BLOCKS):
+            gather(m, D - 1)
+        for m in range(BLOCKS):
+            nc.vector.tensor_tensor(result[m][:], product(m, D - 1), back[m][:], ADD)
+            store(m)

@@ -49,7 +49,7 @@ def tile_picked_agg_lin_relu_sub_l_kernel(tc, xT, w_words, w_scales, b, gate, po
         result = [keep.tile([P, V], F32, name=f"result{m}") for m in range(BLOCKS)]
         warm = keep.tile([P, 8], F32, name="warm")
         acc = [psum.tile([P, n], F32, name=f"acc0_{g}", tag=f"acc0_{g}") for g, (t0, n) in enumerate(GROUPS)]
-        acc1 = psum.tile([P, T], F32, name="acc1", tag="acc1")
+        acc1 = [psum.tile([P, T // 2], F32, name=f"acc1_{h}", tag=f"acc1_{h}") for h in range(2)]
 
         x_rows = xT.rearrange("(a p j) t -> a p j t", p=P, j=PACK)
 
@@ -155,13 +155,14 @@ def tile_picked_agg_lin_relu_sub_l_kernel(tc, xT, w_words, w_scales, b, gate, po
         multiply0(2, 2)
         finish(acc[1], *GROUPS[1], 0)
         finish(acc[2], *GROUPS[2], 0)
-        for a in range(PASSES):
-            multiply(acc1, a, 0, T, 1)
-        finish(acc1, 0, T, 1)
+        for h in range(2):
+            for a in range(PASSES):
+                multiply(acc1[h], a, h * T // 2, T // 2, 1)
+            finish(acc1[h], h * T // 2, T // 2, 1)
 
         back = []
         for m in range(BLOCKS):
-            turned = [psum.tile([P, P], F32, name=f"turned{m}_{h}", tag=f"turned{m}_{h}") for h in range(2)]
+            turned = [psum.tile([P, P], F32, name=f"turned{m}_{h}", tag=f"acc1_{h}" if m == 0 else f"turned{m}_{h}") for h in range(2)]
             for d in range(D - 1):
                 gather(m, d)
                 for h in range(2):

@@ -38,10 +38,11 @@ def tile_picked_agg_lin_relu_sub_l_kernel(tc, xT, w_words, w_scales, b, gate, po
         scales = [keep.tile([P, T], U8, align_bytes=64, name=f"scales{a}") for a in range(PASSES)]
         w_sb = [keep.tile([P, PASSES, P * PACK], U8, align_bytes=64, name=f"w_sb{m}") for m in range(BLOCKS)]
         w_sc = keep.tile([P, PASSES, N], U8, align_bytes=64, name="w_sc")
-        bias = keep.tile([P, BLOCKS], F32, name="bias")
+        columns = keep.tile([P, BLOCKS, 8], F32, name="columns")
         identity = keep.tile([P, P], F32, name="identity")
-        bias_rows = keep.tile([P, P], F32, name="bias_rows")
-        bias_psum = psum.tile([P, P], F32, name="bias_psum", tag="turned1_1")
+        rows = keep.tile([P, V], F32, name="rows")
+        columns_psum = psum.tile([P, BLOCKS, P], F32, name="columns_psum", tag="acc1_0")
+        gates_psum = [psum.tile([P, 2, V], F32, name=f"gates_psum{u}", tag=f"turned1_{u}") for u in range(2)]
         gates = keep.tile([P, D, V], F32, name="gates")
         y = [keep.tile([P, T], F32, name=f"y{m}") for m in range(BLOCKS)]
         picked = [keep.tile([P, D, V], F32, name=f"picked{m}") for m in range(BLOCKS)]
@@ -86,10 +87,10 @@ def tile_picked_agg_lin_relu_sub_l_kernel(tc, xT, w_words, w_scales, b, gate, po
             multiply(acc[g], a, *GROUPS[g], 0)
 
         def finish(bank, t0, n, m):
-            nc.scalar.activation(out=y[m][:, t0 : t0 + n], in_=bank[:], func=RELU, bias=bias[:, m : m + 1], scale=1.0)
+            nc.scalar.activation(out=y[m][:, t0 : t0 + n], in_=bank[:], func=RELU, bias=columns[:, m, D : D + 1], scale=1.0)
 
         def product(m, d):
-            return gates[:, 2, :] if (m, d) == (0, 3) else picked[m][:, d, :]
+            return gates[:, 1, :] if (m, d) == (0, 3) else picked[m][:, d, :]
 
         def gather(m, d):
             nc.vector.tensor_tensor(product(m, d), y[m][:].indirect(lists[d][:]), gates[:, d, :], MULT)
@@ -103,15 +104,13 @@ def tile_picked_agg_lin_relu_sub_l_kernel(tc, xT, w_words, w_scales, b, gate, po
         def load_w(m, a0, a1):
             nc.sync.dma_start(out=w_sb[m][:, a0:a1, :], in_=w_words[a0:a1, :, m * P : (m + 1) * P, :].rearrange("a p n r -> p a (n r)"))
 
-        def load_gate(d0, d1):
-            nc.sync.dma_start(out=gates[:, d0:d1, :], in_=gate[d0:d1, 0:P, :].rearrange("d p v -> p d v"))
-
         def load_list(d):
             nc.sync.dma_start(lists[d][:], (pos1, pos2, pos3, pos4)[d])
 
         make_identity(nc, identity[:])
-        nc.vector.memset(bias_rows[:], 0.0)
-        nc.scalar.dma_start(out=bias_rows[0:BLOCKS, :], in_=b.rearrange("(m p) o -> m (p o)", p=P))
+        nc.vector.memset(rows[:], 0.0)
+        nc.scalar.dma_start(out=rows[0:D, :], in_=gate[:, 0, :])
+        nc.scalar.dma_start(out=rows[D : D + 1, :], in_=b.rearrange("n o -> o n"))
         load(0)
         for q in range(4):
             nc.sync.dma_start(
@@ -123,15 +122,16 @@ def tile_picked_agg_lin_relu_sub_l_kernel(tc, xT, w_words, w_scales, b, gate, po
         for i in range(2, len(CHUNKS)):
             load(i)
         load_w(0, 2, 3)
-        load_list(0)
-        load_list(1)
-        load_gate(0, 2)
+        for d in range(D - 1):
+            load_list(d)
         load_w(1, 0, 3)
-        load_list(2)
-        load_gate(2, 4)
-        load_list(3)
-        nc.tensor.transpose(bias_psum[:], bias_rows[:], identity[:])
-        nc.vector.tensor_copy(out=bias[:], in_=bias_psum[:, 0:BLOCKS])
+        load_list(D - 1)
+        for h in range(2):
+            nc.tensor.transpose(columns_psum[:, h, :], rows[:, h * P : (h + 1) * P], identity[:])
+        nc.vector.tensor_copy(out=columns[:], in_=columns_psum[:, :, 0:8])
+        for d in range(D):
+            for h in range(2):
+                nc.tensor.transpose(gates_psum[d // 2][:, d % 2, h * P : (h + 1) * P], columns[:, h, d : d + 1].to_broadcast([P, P]), identity[:])
 
         nc.scalar.activation(out=warm[:, 0:1], in_=warm[:, 1:2], func=RELU)
 
@@ -141,6 +141,9 @@ def tile_picked_agg_lin_relu_sub_l_kernel(tc, xT, w_words, w_scales, b, gate, po
             quantize(i, 0, 512)
             for g in range(3):
                 multiply0(i, g)
+            if i == 0:
+                for u in range(2):
+                    nc.scalar.copy(out=gates[:, 2 * u : 2 * u + 2, :], in_=gates_psum[u][:])
         interleave(nc.vector.tensor_copy, 2, 0, 128)
         interleave(nc.scalar.copy, 2, 256, 384)
         interleave(nc.vector.tensor_copy, 2, 128, 256)

@@ -14,15 +14,15 @@ U16 = mybir.dt.uint16
 U8 = mybir.dt.uint8
 FP8X4 = mybir.dt.float8_e4m3fn_x4
 RELU = mybir.ActivationFunctionType.Relu
-ADD, MULT = mybir.AluOpType.add, mybir.AluOpType.mult
+ADD, MULT, MAX = mybir.AluOpType.add, mybir.AluOpType.mult, mybir.AluOpType.max
 
 P = 128
 PACK = 4
 PASSES = K // (P * PACK)
 BLOCKS = N // P
 
-CHUNKS = ((0, 0, 512), (1, 0, 512), (2, 0, 384), (2, 384, 128))
-GROUPS = ((0, 128), (128, 256), (384, 128))
+CHUNKS = ((0,0,512),(1,0,256),(1,256,256),(2,0,240),(2,240,128),(2,368,144))
+GROUPS = ((0,128),(128,128),(256,128),(384,128))
 
 
 def tile_picked_agg_lin_relu_sub_l_kernel(tc, xT, w_words, w_scales, b, gate, pos1, pos2, pos3, pos4, out):
@@ -32,19 +32,23 @@ def tile_picked_agg_lin_relu_sub_l_kernel(tc, xT, w_words, w_scales, b, gate, po
         psum = ctx.enter_context(tc.psum_pool(name="psum", bufs=1))
 
         lists = [keep.tile([P, V // 16], U16, name=f"list{d}") for d in range(D)]
-        raw = [keep.tile([P, PACK, n], F32, name=f"raw{i}") for i, (a, t0, n) in enumerate(CHUNKS)]
-        grouped = [keep.tile([P, n, PACK], BF16, align_bytes=64, name=f"grouped{i}") for i, (a, t0, n) in enumerate(CHUNKS)]
+        raw = [keep.tile([P, PACK, n], F32, name=f"raw{i}", tag=f"raw{i}") for i, (a, t0, n) in enumerate(CHUNKS)]
+        grouped = [keep.tile([P, T, PACK], BF16, align_bytes=64, name=f"grouped{a}") for a in range(PASSES - 1)]
+        last = [keep.tile([P, n, PACK], BF16, align_bytes=64, name=f"last{g}") for g, (t0, n) in enumerate(GROUPS)]
+
+        def words(a, c0, c1):
+            if a < PASSES - 1:
+                return grouped[a][:, c0:c1, :]
+            return last[c0 // P][:, c0 % P : c0 % P + c1 - c0, :]
+
         codes = [keep.tile([P, T], U32, align_bytes=64, name=f"codes{a}") for a in range(PASSES)]
         scales = [keep.tile([P, T], U8, align_bytes=64, name=f"scales{a}") for a in range(PASSES)]
         w_sb = [keep.tile([P, PASSES, P * PACK], U8, align_bytes=64, name=f"w_sb{m}") for m in range(BLOCKS)]
         w_sc = keep.tile([P, PASSES, N], U8, align_bytes=64, name="w_sc")
-        columns = keep.tile([P, BLOCKS, 8], F32, name="columns")
         identity = keep.tile([P, P], F32, name="identity")
-        rows = keep.tile([P, V], F32, name="rows")
-        columns_psum = psum.tile([P, BLOCKS, P], F32, name="columns_psum", tag="acc1_0")
-        gates_psum = [psum.tile([P, 2, V], F32, name=f"gates_psum{u}", tag=f"turned1_{u}") for u in range(2)]
+        bias = keep.tile([P, BLOCKS], F32, name="bias")
         gates = keep.tile([P, D, V], F32, name="gates")
-        y = [keep.tile([P, T], F32, name=f"y{m}") for m in range(BLOCKS)]
+        y = [keep.tile([P, T], F32, name=f"y{m}", tag=f"raw{5}" if m == 0 else "y1") for m in range(BLOCKS)]
         picked = [keep.tile([P, D, V], F32, name=f"picked{m}") for m in range(BLOCKS)]
         turned_sb = [[keep.tile([P, P], F32, name=f"turned_sb{m}_{h}") for h in range(2)] for m in range(BLOCKS)]
         result = [keep.tile([P, V], F32, name=f"result{m}") for m in range(BLOCKS)]
@@ -58,18 +62,38 @@ def tile_picked_agg_lin_relu_sub_l_kernel(tc, xT, w_words, w_scales, b, gate, po
             a, t0, n = CHUNKS[i]
             nc.sync.dma_start(out=raw[i][:], in_=x_rows[a][:, :, t0 : t0 + n])
 
+        def load_w(m, a0, a1):
+            nc.sync.dma_start(out=w_sb[m][:, a0:a1, :], in_=w_words[a0:a1, :, m * P : (m + 1) * P, :].rearrange("a p n r -> p a (n r)"))
+
+        def load_list(d):
+            nc.sync.dma_start(lists[d][:], (pos1, pos2, pos3, pos4)[d])
+
+        def load_gate(d0, d1):
+            nc.sync.dma_start(out=gates[:, d0:d1, :], in_=gate[d0:d1, 0:P, :].rearrange("d p v -> p d v"))
+
+        def load_bias():
+            with nc.allow_non_contiguous_dma(reason="one bias value a partition"):
+                nc.sync.dma_start(out=bias[:], in_=b.rearrange("(m p) o -> p (m o)", p=P))
+
+        def load_scales(engine):
+            for q in range(4):
+                engine.dma_start(
+                    out=w_sc[32 * q : 32 * q + 4, :, :].bitcast(I32),
+                    in_=w_scales[:, 4 * q : 4 * q + 4, :].rearrange("a r n -> r a n").bitcast(I32),
+                )
+
         def interleave(copy, i, c0, c1):
+            a, t0, n = CHUNKS[i]
             copy(
-                out=grouped[i][:, c0:c1, :].rearrange("p (c i) j -> p c j i", i=4),
-                in_=raw[i][:, :, c0:c1].rearrange("p j (c i) -> p c j i", i=4),
+                out=words(a, c0, c1).rearrange("p (c i) j -> p c j i", i=4),
+                in_=raw[i][:, :, c0 - t0 : c1 - t0].rearrange("p j (c i) -> p c j i", i=4),
             )
 
-        def quantize(i, c0, c1):
-            a, t0, n = CHUNKS[i]
+        def quantize(a, c0, c1):
             nc.vector.quantize_mx(
-                out=codes[a][:, t0 + c0 : t0 + c1].bitcast(FP8X4),
-                scales=scales[a][:, t0 + c0 : t0 + c1],
-                in_=grouped[i][:, c0:c1, :].rearrange("p c j -> p (c j)"),
+                out=codes[a][:, c0:c1].bitcast(FP8X4),
+                scales=scales[a][:, c0:c1],
+                in_=words(a, c0, c1).rearrange("p c j -> p (c j)"),
             )
 
         def multiply(bank, a, t0, n, m):
@@ -87,7 +111,14 @@ def tile_picked_agg_lin_relu_sub_l_kernel(tc, xT, w_words, w_scales, b, gate, po
             multiply(acc[g], a, *GROUPS[g], 0)
 
         def finish(bank, t0, n, m):
-            nc.scalar.activation(out=y[m][:, t0 : t0 + n], in_=bank[:], func=RELU, bias=columns[:, m, D : D + 1], scale=1.0)
+            nc.scalar.activation(out=y[m][:, t0 : t0 + n], in_=bank[:], func=RELU, bias=bias[:, m : m + 1], scale=1.0)
+
+        def finish0(g):
+            finish(acc[g], *GROUPS[g], 0)
+
+        def finish0_vector(g):
+            t0, n = GROUPS[g]
+            nc.vector.tensor_scalar(out=y[0][:, t0 : t0 + n], in0=acc[g][:], scalar1=bias[:, 0:1], scalar2=0.0, op0=ADD, op1=MAX)
 
         def product(m, d):
             return gates[:, 1, :] if (m, d) == (0, 3) else picked[m][:, d, :]
@@ -95,87 +126,81 @@ def tile_picked_agg_lin_relu_sub_l_kernel(tc, xT, w_words, w_scales, b, gate, po
         def gather(m, d):
             nc.vector.tensor_tensor(product(m, d), y[m][:].indirect(lists[d][:]), gates[:, d, :], MULT)
 
-        def store(m, v0=0, v1=V):
-            nc.sync.dma_start(out=out[m * P : (m + 1) * P, v0:v1], in_=result[m][:, v0:v1])
+        def store(engine, m, v0, v1):
+            engine.dma_start(out=out[m * P : (m + 1) * P, v0:v1], in_=result[m][:, v0:v1])
+
+        vcopy, scopy = nc.vector.tensor_copy, nc.scalar.copy
 
         nc.vector.memset(w_sc[:].rearrange("p a n -> p (a n)").bitcast(I32), 0)
         nc.vector.memset(warm[:], 0.0)
-
-        def load_w(m, a0, a1):
-            nc.sync.dma_start(out=w_sb[m][:, a0:a1, :], in_=w_words[a0:a1, :, m * P : (m + 1) * P, :].rearrange("a p n r -> p a (n r)"))
-
-        def load_list(d):
-            nc.sync.dma_start(lists[d][:], (pos1, pos2, pos3, pos4)[d])
-
         make_identity(nc, identity[:])
-        nc.vector.memset(rows[:], 0.0)
-        nc.scalar.dma_start(out=rows[0:D, :], in_=gate[:, 0, :])
-        nc.scalar.dma_start(out=rows[D : D + 1, :], in_=b.rearrange("n o -> o n"))
         load(0)
-        for q in range(4):
-            nc.sync.dma_start(
-                out=w_sc[32 * q : 32 * q + 4, :, :].bitcast(I32),
-                in_=w_scales[:, 4 * q : 4 * q + 4, :].rearrange("a r n -> r a n").bitcast(I32),
-            )
+        load_scales(nc.sync)
         load(1)
+        load(2)
         load_w(0, 0, 2)
-        for i in range(2, len(CHUNKS)):
+        for i in range(3, len(CHUNKS)):
             load(i)
         load_w(0, 2, 3)
-        for d in range(D - 1):
-            load_list(d)
-        load_w(1, 0, 3)
-        load_list(D - 1)
-        for h in range(2):
-            nc.tensor.transpose(columns_psum[:, h, :], rows[:, h * P : (h + 1) * P], identity[:])
-        nc.vector.tensor_copy(out=columns[:], in_=columns_psum[:, :, 0:8])
-        for d in range(D):
-            for h in range(2):
-                nc.tensor.transpose(gates_psum[d // 2][:, d % 2, h * P : (h + 1) * P], columns[:, h, d : d + 1].to_broadcast([P, P]), identity[:])
+        load_bias()
+        load_w(1, 0, 2)
+        load_list(0)
+        load_gate(0, 2)
+        load_list(1)
+        load_list(2)
+        load_w(1, 2, 3)
+        load_gate(2, 4)
+        load_list(3)
 
         nc.scalar.activation(out=warm[:, 0:1], in_=warm[:, 1:2], func=RELU)
 
-        for i in (0, 1):
-            interleave(nc.vector.tensor_copy, i, 0, 320)
-            interleave(nc.scalar.copy, i, 320, 512)
-            quantize(i, 0, 512)
-            for g in range(3):
-                multiply0(i, g)
-            if i == 0:
-                for u in range(2):
-                    nc.scalar.copy(out=gates[:, 2 * u : 2 * u + 2, :], in_=gates_psum[u][:])
-        interleave(nc.vector.tensor_copy, 2, 0, 128)
-        interleave(nc.scalar.copy, 2, 256, 384)
-        interleave(nc.vector.tensor_copy, 2, 128, 256)
-        interleave(nc.scalar.copy, 3, 64, 128)
-        quantize(2, 0, 128)
-        multiply0(2, 0)
-        interleave(nc.vector.tensor_copy, 3, 0, 64)
-        quantize(2, 128, 384)
-        multiply0(2, 1)
-        finish(acc[0], *GROUPS[0], 0)
-        quantize(3, 0, 128)
-        multiply0(2, 2)
-        finish(acc[1], *GROUPS[1], 0)
-        finish(acc[2], *GROUPS[2], 0)
-        for h in range(2):
-            for a in range(PASSES):
+        interleave(vcopy, 0, 0, 320)
+        interleave(scopy, 0, 320, 512)
+        quantize(0, 0, 512)
+        for g in range(len(GROUPS)):
+            multiply0(0, g)
+        for i in (1, 2):
+            t0 = CHUNKS[i][1]
+            interleave(vcopy, i, t0, t0 + 144)
+            interleave(scopy, i, t0 + 144, t0 + 256)
+            quantize(1, t0, t0 + 256)
+            multiply0(1, 2 * i - 2)
+            multiply0(1, 2 * i - 1)
+        interleave(vcopy, 3, 0, 128)
+        interleave(scopy, 3, 128, 240)
+        interleave(scopy, 4, 240, 256)
+        interleave(vcopy, 4, 256, 320)
+        interleave(scopy, 4, 320, 368)
+        interleave(scopy, 5, 368, 384)
+        interleave(vcopy, 5, 384, 464)
+        interleave(scopy, 5, 464, 512)
+        for g, (t0, n) in enumerate(GROUPS):
+            quantize(2, t0, t0 + n)
+            multiply0(2, g)
+        for g in range(len(GROUPS)):
+            finish0(g)
+        for a in range(PASSES):
+            for h in range(2):
                 multiply(acc1[h], a, h * T // 2, T // 2, 1)
+        for h in range(2):
             finish(acc1[h], h * T // 2, T // 2, 1)
 
-        back = []
+        turned = [[psum.tile([P, P], F32, name=f"turned{m}_{h}", tag=f"acc1_{h}" if m == 0 else f"turned{m}_{h}") for h in range(2)] for m in range(BLOCKS)]
+        back0 = psum.tile([P, V], F32, name="back0", tag="acc0_0")
+        back1 = [psum.tile([P, P], F32, name=f"back1_{h}", tag=f"acc0_{h + 1}") for h in range(2)]
+        back = [[back0[:, 0:P], back0[:, P:V]], [back1[0][:], back1[1][:]]]
         for m in range(BLOCKS):
-            turned = [psum.tile([P, P], F32, name=f"turned{m}_{h}", tag=f"acc1_{h}" if m == 0 else f"turned{m}_{h}") for h in range(2)]
             for d in range(D - 1):
                 gather(m, d)
                 for h in range(2):
-                    nc.tensor.matmul(turned[h][:], lhsT=picked[m][:, d, h * P : (h + 1) * P], rhs=identity[:], is_transpose=True, start=(d == 0), stop=(d == D - 2))
-            back.append(psum.tile([P, V], F32, name=f"back{m}", tag=f"acc0_{m}"))
+                    nc.tensor.matmul(turned[m][h][:], lhsT=picked[m][:, d, h * P : (h + 1) * P], rhs=identity[:], is_transpose=True, start=(d == 0), stop=(d == D - 2))
             for h in range(2):
-                nc.scalar.copy(out=turned_sb[m][h][:], in_=turned[h][:])
-                nc.tensor.transpose(back[m][:, h * P : (h + 1) * P], turned_sb[m][h][:], identity[:])
+                nc.scalar.copy(out=turned_sb[m][h][:], in_=turned[m][h][:])
+                nc.tensor.transpose(back[m][h], turned_sb[m][h][:], identity[:])
         for m in range(BLOCKS):
             gather(m, D - 1)
-        for m in range(BLOCKS):
-            nc.vector.tensor_tensor(result[m][:], product(m, D - 1), back[m][:], ADD)
-            store(m)
+        nc.vector.tensor_tensor(result[0][:], product(0, D - 1), back0[:], ADD)
+        store(nc.sync, 0, 0, V)
+        for h in range(2):
+            nc.vector.tensor_tensor(result[1][:, h * P : (h + 1) * P], picked[1][:, D - 1, h * P : (h + 1) * P], back[1][h], ADD)
+        store(nc.sync, 1, 0, V)

@@ -21,7 +21,7 @@ PACK = 4
 PASSES = K // (P * PACK)
 BLOCKS = N // P
 
-CHUNKS = ((0,0,512),(1,0,256),(1,256,256),(2,0,240),(2,240,128),(2,368,144))
+CHUNKS = ((0,0,512),(1,0,512),(2,0,240),(2,240,128),(2,368,144))
 GROUPS = ((0,128),(128,128),(256,128),(384,128))
 
 
@@ -48,7 +48,7 @@ def tile_picked_agg_lin_relu_sub_l_kernel(tc, xT, w_words, w_scales, b, gate, po
         identity = keep.tile([P, P], F32, name="identity")
         bias = keep.tile([P, BLOCKS], F32, name="bias")
         gates = keep.tile([P, D, V], F32, name="gates")
-        y = [keep.tile([P, T], F32, name=f"y{m}", tag=f"raw{5}" if m == 0 else "y1") for m in range(BLOCKS)]
+        y = [keep.tile([P, T], F32, name=f"y{m}", tag=f"raw{4}" if m == 0 else "y1") for m in range(BLOCKS)]
         picked = [keep.tile([P, D, V], F32, name=f"picked{m}") for m in range(BLOCKS)]
         turned_sb = [[keep.tile([P, P], F32, name=f"turned_sb{m}_{h}") for h in range(2)] for m in range(BLOCKS)]
         result = [keep.tile([P, V], F32, name=f"result{m}") for m in range(BLOCKS)]
@@ -137,9 +137,8 @@ def tile_picked_agg_lin_relu_sub_l_kernel(tc, xT, w_words, w_scales, b, gate, po
         load(0)
         load_scales(nc.sync)
         load(1)
-        load(2)
         load_w(0, 0, 2)
-        for i in range(3, len(CHUNKS)):
+        for i in range(2, len(CHUNKS)):
             load(i)
         load_w(0, 2, 3)
         load_bias()
@@ -159,21 +158,21 @@ def tile_picked_agg_lin_relu_sub_l_kernel(tc, xT, w_words, w_scales, b, gate, po
         quantize(0, 0, 512)
         for g in range(len(GROUPS)):
             multiply0(0, g)
-        for i in (1, 2):
-            t0 = CHUNKS[i][1]
-            interleave(vcopy, i, t0, t0 + 144)
-            interleave(scopy, i, t0 + 144, t0 + 256)
-            quantize(1, t0, t0 + 256)
-            multiply0(1, 2 * i - 2)
-            multiply0(1, 2 * i - 1)
-        interleave(vcopy, 3, 0, 128)
-        interleave(scopy, 3, 128, 240)
-        interleave(scopy, 4, 240, 256)
-        interleave(vcopy, 4, 256, 320)
-        interleave(scopy, 4, 320, 368)
-        interleave(scopy, 5, 368, 384)
-        interleave(vcopy, 5, 384, 464)
-        interleave(scopy, 5, 464, 512)
+        interleave(vcopy, 1, 0, 128)
+        interleave(vcopy, 1, 128, 272)
+        interleave(scopy, 1, 272, 384)
+        interleave(scopy, 1, 384, 512)
+        for g, (t0, n) in enumerate(GROUPS):
+            quantize(1, t0, t0 + n)
+            multiply0(1, g)
+        interleave(vcopy, 2, 0, 128)
+        interleave(scopy, 2, 128, 240)
+        interleave(scopy, 3, 240, 256)
+        interleave(vcopy, 3, 256, 320)
+        interleave(scopy, 3, 320, 368)
+        interleave(scopy, 4, 368, 384)
+        interleave(vcopy, 4, 384, 464)
+        interleave(scopy, 4, 464, 512)
         for g, (t0, n) in enumerate(GROUPS):
             quantize(2, t0, t0 + n)
             multiply0(2, g)

@@ -47,6 +47,8 @@ def tile_picked_agg_lin_relu_sub_l_kernel(tc, xT, w_words, w_scales, b, gate, po
         w_sc = keep.tile([P, PASSES, N], U8, align_bytes=64, name="w_sc")
         identity = keep.tile([P, P], F32, name="identity")
         bias = keep.tile([P, BLOCKS], F32, name="bias")
+        bias_rows = keep.tile([P, P], F32, name="bias_rows")
+        bias_psum = psum.tile([P, P], F32, name="bias_psum", tag="turned1_1")
         gates = keep.tile([P, D, V], F32, name="gates")
         y = [keep.tile([P, T], F32, name=f"y{m}", tag=f"raw{4}" if m == 0 else "y1") for m in range(BLOCKS)]
         picked = [keep.tile([P, D, V], F32, name=f"picked{m}") for m in range(BLOCKS)]
@@ -72,8 +74,10 @@ def tile_picked_agg_lin_relu_sub_l_kernel(tc, xT, w_words, w_scales, b, gate, po
             nc.sync.dma_start(out=gates[:, d0:d1, :], in_=gate[d0:d1, 0:P, :].rearrange("d p v -> p d v"))
 
         def load_bias():
-            with nc.allow_non_contiguous_dma(reason="one bias value a partition"):
-                nc.sync.dma_start(out=bias[:], in_=b.rearrange("(m p) o -> p (m o)", p=P))
+            nc.vector.memset(bias_rows[:], 0.0)
+            nc.scalar.dma_start(out=bias_rows[0:BLOCKS, :], in_=b.rearrange("(m p) o -> m (p o)", p=P))
+            nc.tensor.transpose(bias_psum[:], bias_rows[:], identity[:])
+            nc.vector.tensor_copy(out=bias[:], in_=bias_psum[:, 0:BLOCKS])
 
         def load_scales(engine):
             for q in range(4):
@@ -134,6 +138,7 @@ def tile_picked_agg_lin_relu_sub_l_kernel(tc, xT, w_words, w_scales, b, gate, po
         nc.vector.memset(w_sc[:].rearrange("p a n -> p (a n)").bitcast(I32), 0)
         nc.vector.memset(warm[:], 0.0)
         make_identity(nc, identity[:])
+        load_bias()
         load(0)
         load_scales(nc.sync)
         load(1)
@@ -141,14 +146,14 @@ def tile_picked_agg_lin_relu_sub_l_kernel(tc, xT, w_words, w_scales, b, gate, po
         for i in range(2, len(CHUNKS)):
             load(i)
         load_w(0, 2, 3)
-        load_bias()
-        load_w(1, 0, 2)
         load_list(0)
-        load_gate(0, 2)
+        load_gate(0, 1)
+        load_w(1, 0, 2)
         load_list(1)
+        load_gate(1, 3)
         load_list(2)
         load_w(1, 2, 3)
-        load_gate(2, 4)
+        load_gate(3, 4)
         load_list(3)
 
         nc.scalar.activation(out=warm[:, 0:1], in_=warm[:, 1:2], func=RELU)

@@ -21,7 +21,7 @@ PACK = 4
 PASSES = K // (P * PACK)
 BLOCKS = N // P
 
-CHUNKS = ((0,0,512),(1,0,512),(2,0,240),(2,240,128),(2,368,144))
+CHUNKS = ((0,0,512),(1,0,512),(2,0,256),(2,256,128),(2,384,128))
 GROUPS = ((0,128),(128,128),(256,128),(384,128))
 
 
@@ -151,8 +151,8 @@ def tile_picked_agg_lin_relu_sub_l_kernel(tc, xT, w_words, w_scales, b, gate, po
         load_w(1, 0, 2)
         load_list(1)
         load_gate(1, 3)
-        load_list(2)
         load_w(1, 2, 3)
+        load_list(2)
         load_gate(3, 4)
         load_list(3)
 
@@ -171,11 +171,8 @@ def tile_picked_agg_lin_relu_sub_l_kernel(tc, xT, w_words, w_scales, b, gate, po
             quantize(1, t0, t0 + n)
             multiply0(1, g)
         interleave(vcopy, 2, 0, 128)
-        interleave(scopy, 2, 128, 240)
-        interleave(scopy, 3, 240, 256)
-        interleave(vcopy, 3, 256, 320)
-        interleave(scopy, 3, 320, 368)
-        interleave(scopy, 4, 368, 384)
+        interleave(scopy, 2, 128, 256)
+        interleave(scopy, 3, 256, 384)
         interleave(vcopy, 4, 384, 464)
         interleave(scopy, 4, 464, 512)
         for g, (t0, n) in enumerate(GROUPS):

@@ -54,7 +54,6 @@ def tile_picked_agg_lin_relu_sub_l_kernel(tc, xT, w_words, w_scales, b, gate, po
         picked = [keep.tile([P, D, V], F32, name=f"picked{m}") for m in range(BLOCKS)]
         turned_sb = [[keep.tile([P, P], F32, name=f"turned_sb{m}_{h}") for h in range(2)] for m in range(BLOCKS)]
         result = [keep.tile([P, V], F32, name=f"result{m}") for m in range(BLOCKS)]
-        warm = keep.tile([P, 8], F32, name="warm")
         acc = [psum.tile([P, n], F32, name=f"acc0_{g}", tag=f"acc0_{g}") for g, (t0, n) in enumerate(GROUPS)]
         acc1 = [psum.tile([P, T // 2], F32, name=f"acc1_{h}", tag=f"acc1_{h}") for h in range(2)]
 
@@ -75,7 +74,7 @@ def tile_picked_agg_lin_relu_sub_l_kernel(tc, xT, w_words, w_scales, b, gate, po
 
         def load_bias():
             nc.vector.memset(bias_rows[:], 0.0)
-            nc.scalar.dma_start(out=bias_rows[0:BLOCKS, :], in_=b.rearrange("(m p) o -> m (p o)", p=P))
+            nc.sync.dma_start(out=bias_rows[0:BLOCKS, :], in_=b.rearrange("(m p) o -> m (p o)", p=P))
             nc.tensor.transpose(bias_psum[:], bias_rows[:], identity[:])
             nc.vector.tensor_copy(out=bias[:], in_=bias_psum[:, 0:BLOCKS])
 
@@ -136,10 +135,9 @@ def tile_picked_agg_lin_relu_sub_l_kernel(tc, xT, w_words, w_scales, b, gate, po
         vcopy, scopy = nc.vector.tensor_copy, nc.scalar.copy
 
         nc.vector.memset(w_sc[:].rearrange("p a n -> p (a n)").bitcast(I32), 0)
-        nc.vector.memset(warm[:], 0.0)
         make_identity(nc, identity[:])
-        load_bias()
         load(0)
+        load_bias()
         load_scales(nc.sync)
         load(1)
         load_w(0, 0, 2)
@@ -155,8 +153,6 @@ def tile_picked_agg_lin_relu_sub_l_kernel(tc, xT, w_words, w_scales, b, gate, po
         load_list(2)
         load_gate(3, 4)
         load_list(3)
-
-        nc.scalar.activation(out=warm[:, 0:1], in_=warm[:, 1:2], func=RELU)
 
         interleave(vcopy, 0, 0, 320)
         interleave(scopy, 0, 320, 512)

@@ -32,7 +32,7 @@ def tile_picked_agg_lin_relu_sub_l_kernel(tc, xT, w_words, w_scales, b, gate, po
         psum = ctx.enter_context(tc.psum_pool(name="psum", bufs=1))
 
         lists = [keep.tile([P, V // 16], U16, name=f"list{d}") for d in range(D)]
-        raw = [keep.tile([P, PACK, n], F32, name=f"raw{i}", tag=f"raw{i}") for i, (a, t0, n) in enumerate(CHUNKS)]
+        raw = [keep.tile([P, PACK, n], F32, align_bytes=256, name=f"raw{i}", tag=f"raw{i}") for i, (a, t0, n) in enumerate(CHUNKS)]
         grouped = [keep.tile([P, T, PACK], BF16, align_bytes=64, name=f"grouped{a}") for a in range(PASSES - 1)]
         last = [keep.tile([P, n, PACK], BF16, align_bytes=64, name=f"last{g}") for g, (t0, n) in enumerate(GROUPS)]
 
@@ -43,17 +43,17 @@ def tile_picked_agg_lin_relu_sub_l_kernel(tc, xT, w_words, w_scales, b, gate, po
 
         codes = [keep.tile([P, T], U32, align_bytes=64, name=f"codes{a}") for a in range(PASSES)]
         scales = [keep.tile([P, T], U8, align_bytes=64, name=f"scales{a}") for a in range(PASSES)]
-        w_sb = [keep.tile([P, PASSES, P * PACK], U8, align_bytes=64, name=f"w_sb{m}") for m in range(BLOCKS)]
-        w_sc = keep.tile([P, PASSES, N], U8, align_bytes=64, name="w_sc")
+        w_sb = [keep.tile([P, PASSES, P * PACK], U8, align_bytes=256, name=f"w_sb{m}") for m in range(BLOCKS)]
+        w_sc = keep.tile([P, PASSES, N], U8, align_bytes=256, name="w_sc")
         identity = keep.tile([P, P], F32, name="identity")
         bias = keep.tile([P, BLOCKS], F32, name="bias")
         bias_rows = keep.tile([P, P], F32, name="bias_rows")
         bias_psum = psum.tile([P, P], F32, name="bias_psum", tag="turned1_1")
-        gates = keep.tile([P, D, V], F32, name="gates")
-        y = [keep.tile([P, T], F32, name=f"y{m}", tag=f"raw{4}" if m == 0 else "y1") for m in range(BLOCKS)]
-        picked = [keep.tile([P, D, V], F32, name=f"picked{m}") for m in range(BLOCKS)]
+        gates = keep.tile([P, D, V], F32, align_bytes=256, name="gates")
+        y = [keep.tile([P, T], F32, align_bytes=256, name=f"y{m}", tag=f"raw{4}" if m == 0 else "y1") for m in range(BLOCKS)]
+        picked = [keep.tile([P, D, V], F32, align_bytes=256, name=f"picked{m}") for m in range(BLOCKS)]
         turned_sb = [[keep.tile([P, P], F32, name=f"turned_sb{m}_{h}") for h in range(2)] for m in range(BLOCKS)]
-        result = [keep.tile([P, V], F32, name=f"result{m}") for m in range(BLOCKS)]
+        result = [keep.tile([P, V], F32, align_bytes=256, name=f"result{m}") for m in range(BLOCKS)]
         acc = [psum.tile([P, n], F32, name=f"acc0_{g}", tag=f"acc0_{g}") for g, (t0, n) in enumerate(GROUPS)]
         acc1 = [psum.tile([P, T // 2], F32, name=f"acc1_{h}", tag=f"acc1_{h}") for h in range(2)]
 

@@ -138,8 +138,8 @@ def tile_picked_agg_lin_relu_sub_l_kernel(tc, xT, w_words, w_scales, b, gate, po
         make_identity(nc, identity[:])
         load(0)
         load_bias()
-        load_scales(nc.sync)
         load(1)
+        load_scales(nc.sync)
         load_w(0, 0, 2)
         for i in range(2, len(CHUNKS)):
             load(i)

@@ -14,15 +14,20 @@ U16 = mybir.dt.uint16
 U8 = mybir.dt.uint8
 FP8X4 = mybir.dt.float8_e4m3fn_x4
 RELU = mybir.ActivationFunctionType.Relu
-ADD, MULT, MAX = mybir.AluOpType.add, mybir.AluOpType.mult, mybir.AluOpType.max
+ADD, MULT = mybir.AluOpType.add, mybir.AluOpType.mult
 
 P = 128
 PACK = 4
 PASSES = K // (P * PACK)
+LAST = PASSES - 1
 BLOCKS = N // P
+GROUP = 128
+GROUPS = T // GROUP
+HALVES = V // P
 
-CHUNKS = ((0,0,512),(1,0,512),(2,0,256),(2,256,128),(2,384,128))
-GROUPS = ((0,128),(128,128),(256,128),(384,128))
+LOADS = ((0, 0, 512), (1, 0, 512), (2, 0, 256), (2, 256, 128), (2, 384, 128))
+WHOLE_SPLIT = 272
+END_SPLIT = 464
 
 
 def tile_picked_agg_lin_relu_sub_l_kernel(tc, xT, w_words, w_scales, b, gate, pos1, pos2, pos3, pos4, out):
@@ -32,172 +37,164 @@ def tile_picked_agg_lin_relu_sub_l_kernel(tc, xT, w_words, w_scales, b, gate, po
         psum = ctx.enter_context(tc.psum_pool(name="psum", bufs=1))
 
         lists = [keep.tile([P, V // 16], U16, name=f"list{d}") for d in range(D)]
-        raw = [keep.tile([P, PACK, n], F32, align_bytes=256, name=f"raw{i}", tag=f"raw{i}") for i, (a, t0, n) in enumerate(CHUNKS)]
-        grouped = [keep.tile([P, T, PACK], BF16, align_bytes=64, name=f"grouped{a}") for a in range(PASSES - 1)]
-        last = [keep.tile([P, n, PACK], BF16, align_bytes=64, name=f"last{g}") for g, (t0, n) in enumerate(GROUPS)]
-
-        def words(a, c0, c1):
-            if a < PASSES - 1:
-                return grouped[a][:, c0:c1, :]
-            return last[c0 // P][:, c0 % P : c0 % P + c1 - c0, :]
-
+        raw = [keep.tile([P, PACK, n], F32, name=f"raw{i}", tag=f"raw{i}") for i, (a, t0, n) in enumerate(LOADS)]
+        rounded = [[keep.tile([P, GROUP, PACK], BF16, align_bytes=64, name=f"rounded{a}_{g}") for g in range(GROUPS)] for a in range(PASSES)]
         codes = [keep.tile([P, T], U32, align_bytes=64, name=f"codes{a}") for a in range(PASSES)]
         scales = [keep.tile([P, T], U8, align_bytes=64, name=f"scales{a}") for a in range(PASSES)]
-        w_sb = [keep.tile([P, PASSES, P * PACK], U8, align_bytes=256, name=f"w_sb{m}") for m in range(BLOCKS)]
-        w_sc = keep.tile([P, PASSES, N], U8, align_bytes=256, name="w_sc")
+        w_codes = [keep.tile([P, PASSES, P * PACK], U8, align_bytes=64, name=f"w_codes{m}") for m in range(BLOCKS)]
+        w_scale = keep.tile([P, PASSES, N], U8, align_bytes=64, name="w_scale")
         identity = keep.tile([P, P], F32, name="identity")
-        bias = keep.tile([P, BLOCKS], F32, name="bias")
         bias_rows = keep.tile([P, P], F32, name="bias_rows")
-        bias_psum = psum.tile([P, P], F32, name="bias_psum", tag="turned1_1")
-        gates = keep.tile([P, D, V], F32, align_bytes=256, name="gates")
-        y = [keep.tile([P, T], F32, align_bytes=256, name=f"y{m}", tag=f"raw{4}" if m == 0 else "y1") for m in range(BLOCKS)]
-        picked = [keep.tile([P, D, V], F32, align_bytes=256, name=f"picked{m}") for m in range(BLOCKS)]
-        turned_sb = [[keep.tile([P, P], F32, name=f"turned_sb{m}_{h}") for h in range(2)] for m in range(BLOCKS)]
-        result = [keep.tile([P, V], F32, align_bytes=256, name=f"result{m}") for m in range(BLOCKS)]
-        acc = [psum.tile([P, n], F32, name=f"acc0_{g}", tag=f"acc0_{g}") for g, (t0, n) in enumerate(GROUPS)]
-        acc1 = [psum.tile([P, T // 2], F32, name=f"acc1_{h}", tag=f"acc1_{h}") for h in range(2)]
+        bias = keep.tile([P, BLOCKS], F32, name="bias")
+        gates = keep.tile([P, D, V], F32, name="gates")
+        y = [keep.tile([P, T], F32, name="y0", tag=f"raw{len(LOADS) - 1}"), keep.tile([P, T], F32, name="y1")]
+        products = [keep.tile([P, D, V], F32, name=f"products{m}") for m in range(BLOCKS)]
+        turned_sb = [[keep.tile([P, P], F32, name=f"turned_sb{m}_{h}") for h in range(HALVES)] for m in range(BLOCKS)]
+        result = [keep.tile([P, V], F32, name=f"result{m}") for m in range(BLOCKS)]
+
+        def bank(number, columns, name):
+            return psum.tile([P, columns], F32, name=name, tag=f"bank{number}")
+
+        bias_psum = bank(7, P, "bias_psum")
+        sums0 = [bank(g, GROUP, f"sums0_{g}") for g in range(GROUPS)]
+        sums1 = [bank(GROUPS + h, T // 2, f"sums1_{h}") for h in range(2)]
 
         x_rows = xT.rearrange("(a p j) t -> a p j t", p=P, j=PACK)
 
-        def load(i):
-            a, t0, n = CHUNKS[i]
+        def load_x(i):
+            a, t0, n = LOADS[i]
             nc.sync.dma_start(out=raw[i][:], in_=x_rows[a][:, :, t0 : t0 + n])
 
         def load_w(m, a0, a1):
-            nc.sync.dma_start(out=w_sb[m][:, a0:a1, :], in_=w_words[a0:a1, :, m * P : (m + 1) * P, :].rearrange("a p n r -> p a (n r)"))
+            words = w_words[a0:a1, :, m * P : (m + 1) * P, :].rearrange("a p n r -> p a (n r)")
+            nc.sync.dma_start(out=w_codes[m][:, a0:a1, :], in_=words)
 
         def load_list(d):
             nc.sync.dma_start(lists[d][:], (pos1, pos2, pos3, pos4)[d])
 
-        def load_gate(d0, d1):
+        def load_gates(d0, d1):
             nc.sync.dma_start(out=gates[:, d0:d1, :], in_=gate[d0:d1, 0:P, :].rearrange("d p v -> p d v"))
 
-        def load_bias():
-            nc.vector.memset(bias_rows[:], 0.0)
-            nc.sync.dma_start(out=bias_rows[0:BLOCKS, :], in_=b.rearrange("(m p) o -> m (p o)", p=P))
-            nc.tensor.transpose(bias_psum[:], bias_rows[:], identity[:])
-            nc.vector.tensor_copy(out=bias[:], in_=bias_psum[:, 0:BLOCKS])
-
-        def load_scales(engine):
-            for q in range(4):
-                engine.dma_start(
-                    out=w_sc[32 * q : 32 * q + 4, :, :].bitcast(I32),
-                    in_=w_scales[:, 4 * q : 4 * q + 4, :].rearrange("a r n -> r a n").bitcast(I32),
-                )
-
-        def interleave(copy, i, c0, c1):
-            a, t0, n = CHUNKS[i]
+        def interleave(copy, i, t0, t1):
+            a, first, n = LOADS[i]
+            g = t0 // GROUP
             copy(
-                out=words(a, c0, c1).rearrange("p (c i) j -> p c j i", i=4),
-                in_=raw[i][:, :, c0 - t0 : c1 - t0].rearrange("p j (c i) -> p c j i", i=4),
+                out=rounded[a][g][:, t0 - g * GROUP : t1 - g * GROUP, :].rearrange("p (c i) j -> p c j i", i=4),
+                in_=raw[i][:, :, t0 - first : t1 - first].rearrange("p j (c i) -> p c j i", i=4),
             )
 
-        def quantize(a, c0, c1):
+        def quantize(a, g):
+            nodes = slice(g * GROUP, (g + 1) * GROUP)
             nc.vector.quantize_mx(
-                out=codes[a][:, c0:c1].bitcast(FP8X4),
-                scales=scales[a][:, c0:c1],
-                in_=words(a, c0, c1).rearrange("p c j -> p (c j)"),
+                out=codes[a][:, nodes].bitcast(FP8X4),
+                scales=scales[a][:, nodes],
+                in_=rounded[a][g][:].rearrange("p c j -> p (c j)"),
             )
 
-        def multiply(bank, a, t0, n, m):
+        def multiply(sums, m, a, nodes):
             nc.tensor.matmul_mx(
-                out=bank[:],
-                lhsT=w_sb[m][:, a, :].bitcast(FP8X4),
-                lhsT_scale=w_sc[:, a, m * P : (m + 1) * P],
-                rhs=codes[a][:, t0 : t0 + n].bitcast(FP8X4),
-                rhs_scale=scales[a][:, t0 : t0 + n],
+                out=sums[:],
+                lhsT=w_codes[m][:, a, :].bitcast(FP8X4),
+                lhsT_scale=w_scale[:, a, m * P : (m + 1) * P],
+                rhs=codes[a][:, nodes].bitcast(FP8X4),
+                rhs_scale=scales[a][:, nodes],
                 start=(a == 0),
-                stop=(a == PASSES - 1),
+                stop=(a == LAST),
             )
 
-        def multiply0(a, g):
-            multiply(acc[g], a, *GROUPS[g], 0)
-
-        def finish(bank, t0, n, m):
-            nc.scalar.activation(out=y[m][:, t0 : t0 + n], in_=bank[:], func=RELU, bias=bias[:, m : m + 1], scale=1.0)
-
-        def finish0(g):
-            finish(acc[g], *GROUPS[g], 0)
-
-        def finish0_vector(g):
-            t0, n = GROUPS[g]
-            nc.vector.tensor_scalar(out=y[0][:, t0 : t0 + n], in0=acc[g][:], scalar1=bias[:, 0:1], scalar2=0.0, op0=ADD, op1=MAX)
+        def finish(sums, m, nodes):
+            nc.scalar.activation(out=y[m][:, nodes], in_=sums[:], func=RELU, bias=bias[:, m : m + 1], scale=1.0)
 
         def product(m, d):
-            return gates[:, 1, :] if (m, d) == (0, 3) else picked[m][:, d, :]
+            return gates[:, 1, :] if (m, d) == (0, D - 1) else products[m][:, d, :]
 
         def gather(m, d):
             nc.vector.tensor_tensor(product(m, d), y[m][:].indirect(lists[d][:]), gates[:, d, :], MULT)
 
-        def store(engine, m, v0, v1):
-            engine.dma_start(out=out[m * P : (m + 1) * P, v0:v1], in_=result[m][:, v0:v1])
-
-        vcopy, scopy = nc.vector.tensor_copy, nc.scalar.copy
-
-        nc.vector.memset(w_sc[:].rearrange("p a n -> p (a n)").bitcast(I32), 0)
+        nc.vector.memset(w_scale[:].rearrange("p a n -> p (a n)").bitcast(I32), 0)
+        nc.vector.memset(bias_rows[:], 0.0)
         make_identity(nc, identity[:])
-        load(0)
-        load_bias()
-        load(1)
-        load_scales(nc.sync)
-        load_w(0, 0, 2)
-        for i in range(2, len(CHUNKS)):
-            load(i)
-        load_w(0, 2, 3)
+
+        load_x(0)
+        nc.sync.dma_start(out=bias_rows[0:BLOCKS, :], in_=b.rearrange("(m p) o -> m (p o)", p=P))
+        load_x(1)
+        for q in range(4):
+            nc.sync.dma_start(
+                out=w_scale[32 * q : 32 * q + 4, :, :].bitcast(I32),
+                in_=w_scales[:, 4 * q : 4 * q + 4, :].rearrange("a r n -> r a n").bitcast(I32),
+            )
+        load_w(0, 0, LAST)
+        for i in range(LAST, len(LOADS)):
+            load_x(i)
+        load_w(0, LAST, PASSES)
         load_list(0)
-        load_gate(0, 1)
-        load_w(1, 0, 2)
+        load_gates(0, 1)
+        load_w(1, 0, LAST)
         load_list(1)
-        load_gate(1, 3)
-        load_w(1, 2, 3)
+        load_gates(1, 3)
+        load_w(1, LAST, PASSES)
         load_list(2)
-        load_gate(3, 4)
+        load_gates(3, 4)
         load_list(3)
 
-        interleave(vcopy, 0, 0, 320)
-        interleave(scopy, 0, 320, 512)
-        quantize(0, 0, 512)
-        for g in range(len(GROUPS)):
-            multiply0(0, g)
-        interleave(vcopy, 1, 0, 128)
-        interleave(vcopy, 1, 128, 272)
-        interleave(scopy, 1, 272, 384)
-        interleave(scopy, 1, 384, 512)
-        for g, (t0, n) in enumerate(GROUPS):
-            quantize(1, t0, t0 + n)
-            multiply0(1, g)
-        interleave(vcopy, 2, 0, 128)
-        interleave(scopy, 2, 128, 256)
-        interleave(scopy, 3, 256, 384)
-        interleave(vcopy, 4, 384, 464)
-        interleave(scopy, 4, 464, 512)
-        for g, (t0, n) in enumerate(GROUPS):
-            quantize(2, t0, t0 + n)
-            multiply0(2, g)
-        for g in range(len(GROUPS)):
-            finish0(g)
+        nc.tensor.transpose(bias_psum[:], bias_rows[:], identity[:])
+        nc.vector.tensor_copy(out=bias[:], in_=bias_psum[:, 0:BLOCKS])
+
+        by_vector, by_scalar = nc.vector.tensor_copy, nc.scalar.copy
+        groups = [slice(g * GROUP, (g + 1) * GROUP) for g in range(GROUPS)]
+
+        def block0_pass(a):
+            for g in range(GROUPS):
+                quantize(a, g)
+                multiply(sums0[g], 0, a, groups[g])
+
+        for a in range(LAST):
+            interleave(by_vector, a, 0, GROUP)
+            interleave(by_vector, a, GROUP, 2 * GROUP)
+            interleave(by_vector, a, 2 * GROUP, WHOLE_SPLIT)
+            interleave(by_scalar, a, WHOLE_SPLIT, 3 * GROUP)
+            interleave(by_scalar, a, 3 * GROUP, T)
+            block0_pass(a)
+        interleave(by_vector, LAST, 0, GROUP)
+        interleave(by_scalar, LAST, GROUP, 2 * GROUP)
+        interleave(by_scalar, LAST + 1, 2 * GROUP, 3 * GROUP)
+        interleave(by_vector, LAST + 2, 3 * GROUP, END_SPLIT)
+        interleave(by_scalar, LAST + 2, END_SPLIT, T)
+        block0_pass(LAST)
+        for g in range(GROUPS):
+            finish(sums0[g], 0, groups[g])
+
+        node_halves = [slice(h * T // 2, (h + 1) * T // 2) for h in range(2)]
         for a in range(PASSES):
             for h in range(2):
-                multiply(acc1[h], a, h * T // 2, T // 2, 1)
+                multiply(sums1[h], 1, a, node_halves[h])
         for h in range(2):
-            finish(acc1[h], h * T // 2, T // 2, 1)
+            finish(sums1[h], 1, node_halves[h])
 
-        turned = [[psum.tile([P, P], F32, name=f"turned{m}_{h}", tag=f"acc1_{h}" if m == 0 else f"turned{m}_{h}") for h in range(2)] for m in range(BLOCKS)]
-        back0 = psum.tile([P, V], F32, name="back0", tag="acc0_0")
-        back1 = [psum.tile([P, P], F32, name=f"back1_{h}", tag=f"acc0_{h + 1}") for h in range(2)]
-        back = [[back0[:, 0:P], back0[:, P:V]], [back1[0][:], back1[1][:]]]
+        turned = [[bank(GROUPS + HALVES * m + h, P, f"turned{m}_{h}") for h in range(HALVES)] for m in range(BLOCKS)]
+        targets = [slice(h * P, (h + 1) * P) for h in range(HALVES)]
+        back0 = bank(0, V, "back0")
+        back = [[back0[:, half] for half in targets], [bank(1 + h, P, f"back1_{h}")[:] for h in range(HALVES)]]
         for m in range(BLOCKS):
             for d in range(D - 1):
                 gather(m, d)
-                for h in range(2):
-                    nc.tensor.matmul(turned[m][h][:], lhsT=picked[m][:, d, h * P : (h + 1) * P], rhs=identity[:], is_transpose=True, start=(d == 0), stop=(d == D - 2))
-            for h in range(2):
+                for h in range(HALVES):
+                    nc.tensor.matmul(
+                        turned[m][h][:],
+                        lhsT=products[m][:, d, targets[h]],
+                        rhs=identity[:],
+                        is_transpose=True,
+                        start=(d == 0),
+                        stop=(d == D - 2),
+                    )
+            for h in range(HALVES):
                 nc.scalar.copy(out=turned_sb[m][h][:], in_=turned[m][h][:])
                 nc.tensor.transpose(back[m][h], turned_sb[m][h][:], identity[:])
+
         for m in range(BLOCKS):
             gather(m, D - 1)
         nc.vector.tensor_tensor(result[0][:], product(0, D - 1), back0[:], ADD)
-        store(nc.sync, 0, 0, V)
-        for h in range(2):
-            nc.vector.tensor_tensor(result[1][:, h * P : (h + 1) * P], picked[1][:, D - 1, h * P : (h + 1) * P], back[1][h], ADD)
-        store(nc.sync, 1, 0, V)
+        nc.sync.dma_start(out=out[0:P, :], in_=result[0][:])
+        for h in range(HALVES):
+            nc.vector.tensor_tensor(result[1][:, targets[h]], product(1, D - 1)[:, targets[h]], back[1][h], ADD)
+        nc.sync.dma_start(out=out[P:N, :], in_=result[1][:])

@@ -26,7 +26,8 @@ GROUPS = T // GROUP
 HALVES = V // P
 
 LOADS = ((0, 0, 512), (1, 0, 512), (2, 0, 256), (2, 256, 128), (2, 384, 128))
-WHOLE_SPLIT = 272
+FIRST_SPLIT = 320
+SECOND_SPLIT = 272
 END_SPLIT = 464
 
 
@@ -38,7 +39,15 @@ def tile_picked_agg_lin_relu_sub_l_kernel(tc, xT, w_words, w_scales, b, gate, po
 
         lists = [keep.tile([P, V // 16], U16, name=f"list{d}") for d in range(D)]
         raw = [keep.tile([P, PACK, n], F32, name=f"raw{i}", tag=f"raw{i}") for i, (a, t0, n) in enumerate(LOADS)]
-        rounded = [[keep.tile([P, GROUP, PACK], BF16, align_bytes=64, name=f"rounded{a}_{g}") for g in range(GROUPS)] for a in range(PASSES)]
+        whole = [keep.tile([P, T, PACK], BF16, align_bytes=64, name=f"whole{a}") for a in range(LAST)]
+        pieces = [keep.tile([P, GROUP, PACK], BF16, align_bytes=64, name=f"piece{g}") for g in range(GROUPS)]
+
+        def rounded(a, t0, t1):
+            if a < LAST:
+                return whole[a][:, t0:t1, :]
+            g = t0 // GROUP
+            return pieces[g][:, t0 - g * GROUP : t1 - g * GROUP, :]
+
         codes = [keep.tile([P, T], U32, align_bytes=64, name=f"codes{a}") for a in range(PASSES)]
         scales = [keep.tile([P, T], U8, align_bytes=64, name=f"scales{a}") for a in range(PASSES)]
         w_codes = [keep.tile([P, PASSES, P * PACK], U8, align_bytes=64, name=f"w_codes{m}") for m in range(BLOCKS)]
@@ -77,18 +86,16 @@ def tile_picked_agg_lin_relu_sub_l_kernel(tc, xT, w_words, w_scales, b, gate, po
 
         def interleave(copy, i, t0, t1):
             a, first, n = LOADS[i]
-            g = t0 // GROUP
             copy(
-                out=rounded[a][g][:, t0 - g * GROUP : t1 - g * GROUP, :].rearrange("p (c i) j -> p c j i", i=4),
+                out=rounded(a, t0, t1).rearrange("p (c i) j -> p c j i", i=4),
                 in_=raw[i][:, :, t0 - first : t1 - first].rearrange("p j (c i) -> p c j i", i=4),
             )
 
-        def quantize(a, g):
-            nodes = slice(g * GROUP, (g + 1) * GROUP)
+        def quantize(a, nodes):
             nc.vector.quantize_mx(
                 out=codes[a][:, nodes].bitcast(FP8X4),
                 scales=scales[a][:, nodes],
-                in_=rounded[a][g][:].rearrange("p c j -> p (c j)"),
+                in_=rounded(a, nodes.start, nodes.stop).rearrange("p c j -> p (c j)"),
             )
 
         def multiply(sums, m, a, nodes):
@@ -145,16 +152,19 @@ def tile_picked_agg_lin_relu_sub_l_kernel(tc, xT, w_words, w_scales, b, gate, po
 
         def block0_pass(a):
             for g in range(GROUPS):
-                quantize(a, g)
+                quantize(a, groups[g])
                 multiply(sums0[g], 0, a, groups[g])
 
-        for a in range(LAST):
-            interleave(by_vector, a, 0, GROUP)
-            interleave(by_vector, a, GROUP, 2 * GROUP)
-            interleave(by_vector, a, 2 * GROUP, WHOLE_SPLIT)
-            interleave(by_scalar, a, WHOLE_SPLIT, 3 * GROUP)
-            interleave(by_scalar, a, 3 * GROUP, T)
-            block0_pass(a)
+        interleave(by_vector, 0, 0, FIRST_SPLIT)
+        interleave(by_scalar, 0, FIRST_SPLIT, T)
+        quantize(0, slice(0, T))
+        for g in range(GROUPS):
+            multiply(sums0[g], 0, 0, groups[g])
+        interleave(by_vector, 1, 0, GROUP)
+        interleave(by_vector, 1, GROUP, SECOND_SPLIT)
+        interleave(by_scalar, 1, SECOND_SPLIT, 3 * GROUP)
+        interleave(by_scalar, 1, 3 * GROUP, T)
+        block0_pass(1)
         interleave(by_vector, LAST, 0, GROUP)
         interleave(by_scalar, LAST, GROUP, 2 * GROUP)
         interleave(by_scalar, LAST + 1, 2 * GROUP, 3 * GROUP)

@@ -38,9 +38,9 @@ def tile_picked_agg_lin_relu_sub_l_kernel(tc, xT, w_words, w_scales, b, gate, po
         psum = ctx.enter_context(tc.psum_pool(name="psum", bufs=1))
 
         lists = [keep.tile([P, V // 16], U16, name=f"list{d}") for d in range(D)]
-        raw = [keep.tile([P, PACK, n], F32, name=f"raw{i}", tag=f"raw{i}") for i, (a, t0, n) in enumerate(LOADS)]
-        whole = [keep.tile([P, T, PACK], BF16, align_bytes=64, name=f"whole{a}") for a in range(LAST)]
-        pieces = [keep.tile([P, GROUP, PACK], BF16, align_bytes=64, name=f"piece{g}") for g in range(GROUPS)]
+        raw = [keep.tile([P, PACK, n], F32, align_bytes=256, name=f"raw{i}", tag=f"raw{i}") for i, (a, t0, n) in enumerate(LOADS)]
+        whole = [keep.tile([P, T, PACK], BF16, align_bytes=256, name=f"whole{a}") for a in range(LAST)]
+        pieces = [keep.tile([P, GROUP, PACK], BF16, align_bytes=256, name=f"piece{g}") for g in range(GROUPS)]
 
         def rounded(a, t0, t1):
             if a < LAST:
@@ -48,18 +48,18 @@ def tile_picked_agg_lin_relu_sub_l_kernel(tc, xT, w_words, w_scales, b, gate, po
             g = t0 // GROUP
             return pieces[g][:, t0 - g * GROUP : t1 - g * GROUP, :]
 
-        codes = [keep.tile([P, T], U32, align_bytes=64, name=f"codes{a}") for a in range(PASSES)]
-        scales = [keep.tile([P, T], U8, align_bytes=64, name=f"scales{a}") for a in range(PASSES)]
-        w_codes = [keep.tile([P, PASSES, P * PACK], U8, align_bytes=64, name=f"w_codes{m}") for m in range(BLOCKS)]
-        w_scale = keep.tile([P, PASSES, N], U8, align_bytes=64, name="w_scale")
-        identity = keep.tile([P, P], F32, name="identity")
+        codes = [keep.tile([P, T], U32, align_bytes=256, name=f"codes{a}") for a in range(PASSES)]
+        scales = [keep.tile([P, T], U8, align_bytes=256, name=f"scales{a}") for a in range(PASSES)]
+        w_codes = [keep.tile([P, PASSES, P * PACK], U8, align_bytes=256, name=f"w_codes{m}") for m in range(BLOCKS)]
+        w_scale = keep.tile([P, PASSES, N], U8, align_bytes=256, name="w_scale")
+        identity = keep.tile([P, P], F32, align_bytes=256, name="identity")
         bias_rows = keep.tile([P, P], F32, name="bias_rows")
         bias = keep.tile([P, BLOCKS], F32, name="bias")
-        gates = keep.tile([P, D, V], F32, name="gates")
-        y = [keep.tile([P, T], F32, name="y0", tag=f"raw{len(LOADS) - 1}"), keep.tile([P, T], F32, name="y1")]
-        products = [keep.tile([P, D, V], F32, name=f"products{m}") for m in range(BLOCKS)]
-        turned_sb = [[keep.tile([P, P], F32, name=f"turned_sb{m}_{h}") for h in range(HALVES)] for m in range(BLOCKS)]
-        result = [keep.tile([P, V], F32, name=f"result{m}") for m in range(BLOCKS)]
+        gates = keep.tile([P, D, V], F32, align_bytes=256, name="gates")
+        y = [keep.tile([P, T], F32, align_bytes=256, name="y0", tag=f"raw{len(LOADS) - 1}"), keep.tile([P, T], F32, align_bytes=256, name="y1")]
+        products = [keep.tile([P, D, V], F32, align_bytes=256, name=f"products{m}") for m in range(BLOCKS)]
+        turned_sb = [[keep.tile([P, P], F32, align_bytes=256, name=f"turned_sb{m}_{h}") for h in range(HALVES)] for m in range(BLOCKS)]
+        result = [keep.tile([P, V], F32, align_bytes=256, name=f"result{m}") for m in range(BLOCKS)]
 
         def bank(number, columns, name):
             return psum.tile([P, columns], F32, name=name, tag=f"bank{number}")

@@ -26,7 +26,6 @@ GROUPS = T // GROUP
 HALVES = V // P
 
 LOADS = ((0, 0, 512), (1, 0, 512), (2, 0, 256), (2, 256, 128), (2, 384, 128))
-FIRST_SPLIT = 320
 SECOND_SPLIT = 272
 END_SPLIT = 464
 
@@ -122,7 +121,8 @@ def tile_picked_agg_lin_relu_sub_l_kernel(tc, xT, w_words, w_scales, b, gate, po
         nc.vector.memset(bias_rows[:], 0.0)
         make_identity(nc, identity[:])
 
-        load_x(0)
+        for queue, rows in ((nc.sync, slice(0, 2)), (nc.scalar, slice(2, 4))):
+            queue.dma_start(out=raw[0][:, rows, :], in_=x_rows[0][:, rows, :])
         nc.sync.dma_start(out=bias_rows[0:BLOCKS, :], in_=b.rearrange("(m p) o -> m (p o)", p=P))
         load_x(1)
         for q in range(4):
@@ -155,8 +155,7 @@ def tile_picked_agg_lin_relu_sub_l_kernel(tc, xT, w_words, w_scales, b, gate, po
                 quantize(a, groups[g])
                 multiply(sums0[g], 0, a, groups[g])
 
-        interleave(by_vector, 0, 0, FIRST_SPLIT)
-        interleave(by_scalar, 0, FIRST_SPLIT, T)
+        interleave(by_vector, 0, 0, T)
         quantize(0, slice(0, T))
         for g in range(GROUPS):
             multiply(sums0[g], 0, 0, groups[g])

@@ -36,7 +36,7 @@ def tile_picked_agg_lin_relu_sub_l_kernel(tc, xT, w_words, w_scales, b, gate, po
         keep = ctx.enter_context(tc.tile_pool(name="keep", bufs=1))
         psum = ctx.enter_context(tc.psum_pool(name="psum", bufs=1))
 
-        lists = [keep.tile([P, V // 16], U16, name=f"list{d}") for d in range(D)]
+        lists = [keep.tile([P, V // 16], U16, align_bytes=256, name=f"list{d}") for d in range(D)]
         raw = [keep.tile([P, PACK, n], F32, align_bytes=256, name=f"raw{i}", tag=f"raw{i}") for i, (a, t0, n) in enumerate(LOADS)]
         whole = [keep.tile([P, T, PACK], BF16, align_bytes=256, name=f"whole{a}") for a in range(LAST)]
         pieces = [keep.tile([P, GROUP, PACK], BF16, align_bytes=256, name=f"piece{g}") for g in range(GROUPS)]
@@ -52,8 +52,8 @@ def tile_picked_agg_lin_relu_sub_l_kernel(tc, xT, w_words, w_scales, b, gate, po
         w_codes = [keep.tile([P, PASSES, P * PACK], U8, align_bytes=256, name=f"w_codes{m}") for m in range(BLOCKS)]
         w_scale = keep.tile([P, PASSES, N], U8, align_bytes=256, name="w_scale")
         identity = keep.tile([P, P], F32, align_bytes=256, name="identity")
-        bias_rows = keep.tile([P, P], F32, name="bias_rows")
-        bias = keep.tile([P, BLOCKS], F32, name="bias")
+        bias_rows = keep.tile([P, P], F32, align_bytes=256, name="bias_rows")
+        bias = keep.tile([P, BLOCKS], F32, align_bytes=256, name="bias")
         gates = keep.tile([P, D, V], F32, align_bytes=256, name="gates")
         y = [keep.tile([P, T], F32, align_bytes=256, name="y0", tag=f"raw{len(LOADS) - 1}"), keep.tile([P, T], F32, align_bytes=256, name="y1")]
         products = [keep.tile([P, D, V], F32, align_bytes=256, name=f"products{m}") for m in range(BLOCKS)]

@@ -24,9 +24,11 @@ BLOCKS = N // P
 GROUP = 128
 GROUPS = T // GROUP
 HALVES = V // P
+RUN = 4
+QUADRANT = 32
+ALIGN = 256
 
 LOADS = ((0, 0, 512), (1, 0, 512), (2, 0, 256), (2, 256, 128), (2, 384, 128))
-SECOND_SPLIT = 272
 END_SPLIT = 464
 
 
@@ -36,10 +38,10 @@ def tile_picked_agg_lin_relu_sub_l_kernel(tc, xT, w_words, w_scales, b, gate, po
         keep = ctx.enter_context(tc.tile_pool(name="keep", bufs=1))
         psum = ctx.enter_context(tc.psum_pool(name="psum", bufs=1))
 
-        lists = [keep.tile([P, V // 16], U16, align_bytes=256, name=f"list{d}") for d in range(D)]
-        raw = [keep.tile([P, PACK, n], F32, align_bytes=256, name=f"raw{i}", tag=f"raw{i}") for i, (a, t0, n) in enumerate(LOADS)]
-        whole = [keep.tile([P, T, PACK], BF16, align_bytes=256, name=f"whole{a}") for a in range(LAST)]
-        pieces = [keep.tile([P, GROUP, PACK], BF16, align_bytes=256, name=f"piece{g}") for g in range(GROUPS)]
+        lists = [keep.tile([P, V // 16], U16, align_bytes=ALIGN, name=f"list{d}") for d in range(D)]
+        raw = [keep.tile([P, PACK, n], F32, align_bytes=ALIGN, name=f"raw{i}", tag=f"raw{i}") for i, (a, t0, n) in enumerate(LOADS)]
+        whole = [keep.tile([P, T, PACK], BF16, align_bytes=ALIGN, name=f"whole{a}") for a in range(LAST)]
+        pieces = [keep.tile([P, GROUP, PACK], BF16, align_bytes=ALIGN, name=f"piece{g}") for g in range(GROUPS)]
 
         def rounded(a, t0, t1):
             if a < LAST:
@@ -47,18 +49,18 @@ def tile_picked_agg_lin_relu_sub_l_kernel(tc, xT, w_words, w_scales, b, gate, po
             g = t0 // GROUP
             return pieces[g][:, t0 - g * GROUP : t1 - g * GROUP, :]
 
-        codes = [keep.tile([P, T], U32, align_bytes=256, name=f"codes{a}") for a in range(PASSES)]
-        scales = [keep.tile([P, T], U8, align_bytes=256, name=f"scales{a}") for a in range(PASSES)]
-        w_codes = [keep.tile([P, PASSES, P * PACK], U8, align_bytes=256, name=f"w_codes{m}") for m in range(BLOCKS)]
-        w_scale = keep.tile([P, PASSES, N], U8, align_bytes=256, name="w_scale")
-        identity = keep.tile([P, P], F32, align_bytes=256, name="identity")
-        bias_rows = keep.tile([P, P], F32, align_bytes=256, name="bias_rows")
-        bias = keep.tile([P, BLOCKS], F32, align_bytes=256, name="bias")
-        gates = keep.tile([P, D, V], F32, align_bytes=256, name="gates")
-        y = [keep.tile([P, T], F32, align_bytes=256, name="y0", tag=f"raw{len(LOADS) - 1}"), keep.tile([P, T], F32, align_bytes=256, name="y1")]
-        products = [keep.tile([P, D, V], F32, align_bytes=256, name=f"products{m}") for m in range(BLOCKS)]
-        turned_sb = [[keep.tile([P, P], F32, align_bytes=256, name=f"turned_sb{m}_{h}") for h in range(HALVES)] for m in range(BLOCKS)]
-        result = [keep.tile([P, V], F32, align_bytes=256, name=f"result{m}") for m in range(BLOCKS)]
+        codes = [keep.tile([P, T], U32, align_bytes=ALIGN, name=f"codes{a}") for a in range(PASSES)]
+        scales = [keep.tile([P, T], U8, align_bytes=ALIGN, name=f"scales{a}") for a in range(PASSES)]
+        w_codes = [keep.tile([P, PASSES, P * PACK], U8, align_bytes=ALIGN, name=f"w_codes{m}") for m in range(BLOCKS)]
+        w_scale = keep.tile([P, PASSES, N], U8, align_bytes=ALIGN, name="w_scale")
+        identity = keep.tile([P, P], F32, align_bytes=ALIGN, name="identity")
+        bias_rows = keep.tile([P, P], F32, align_bytes=ALIGN, name="bias_rows")
+        bias = keep.tile([P, BLOCKS], F32, align_bytes=ALIGN, name="bias")
+        gates = keep.tile([P, D, V], F32, align_bytes=ALIGN, name="gates")
+        y = [keep.tile([P, T], F32, align_bytes=ALIGN, name="y0", tag=f"raw{len(LOADS) - 1}"), keep.tile([P, T], F32, align_bytes=ALIGN, name="y1")]
+        products = [keep.tile([P, D, V], F32, align_bytes=ALIGN, name=f"products{m}") for m in range(BLOCKS)]
+        turned_sb = [[keep.tile([P, P], F32, align_bytes=ALIGN, name=f"turned_sb{m}_{h}") for h in range(HALVES)] for m in range(BLOCKS)]
+        result = [keep.tile([P, V], F32, align_bytes=ALIGN, name=f"result{m}") for m in range(BLOCKS)]
 
         def bank(number, columns, name):
             return psum.tile([P, columns], F32, name=name, tag=f"bank{number}")
@@ -86,8 +88,8 @@ def tile_picked_agg_lin_relu_sub_l_kernel(tc, xT, w_words, w_scales, b, gate, po
         def interleave(copy, i, t0, t1):
             a, first, n = LOADS[i]
             copy(
-                out=rounded(a, t0, t1).rearrange("p (c i) j -> p c j i", i=4),
-                in_=raw[i][:, :, t0 - first : t1 - first].rearrange("p j (c i) -> p c j i", i=4),
+                out=rounded(a, t0, t1).rearrange("p (c s) j -> p c j s", s=RUN),
+                in_=raw[i][:, :, t0 - first : t1 - first].rearrange("p j (c s) -> p c j s", s=RUN),
             )
 
         def quantize(a, nodes):
@@ -125,9 +127,9 @@ def tile_picked_agg_lin_relu_sub_l_kernel(tc, xT, w_words, w_scales, b, gate, po
             queue.dma_start(out=raw[0][:, rows, :], in_=x_rows[0][:, rows, :])
         nc.sync.dma_start(out=bias_rows[0:BLOCKS, :], in_=b.rearrange("(m p) o -> m (p o)", p=P))
         load_x(1)
-        for q in range(4):
+        for q in range(P // QUADRANT):
             nc.sync.dma_start(
-                out=w_scale[32 * q : 32 * q + 4, :, :].bitcast(I32),
+                out=w_scale[QUADRANT * q : QUADRANT * q + 4, :, :].bitcast(I32),
                 in_=w_scales[:, 4 * q : 4 * q + 4, :].rearrange("a r n -> r a n").bitcast(I32),
             )
         load_w(0, 0, LAST)
@@ -160,8 +162,8 @@ def tile_picked_agg_lin_relu_sub_l_kernel(tc, xT, w_words, w_scales, b, gate, po
         for g in range(GROUPS):
             multiply(sums0[g], 0, 0, groups[g])
         interleave(by_vector, 1, 0, GROUP)
-        interleave(by_vector, 1, GROUP, SECOND_SPLIT)
-        interleave(by_scalar, 1, SECOND_SPLIT, 3 * GROUP)
+        interleave(by_vector, 1, GROUP, 2 * GROUP)
+        interleave(by_scalar, 1, 2 * GROUP, 3 * GROUP)
         interleave(by_scalar, 1, 3 * GROUP, T)
         block0_pass(1)
         interleave(by_vector, LAST, 0, GROUP)

@@ -29,7 +29,8 @@ QUADRANT = 32
 ALIGN = 256
 
 LOADS = ((0, 0, 512), (1, 0, 512), (2, 0, 256), (2, 256, 128), (2, 384, 128))
-END_SPLIT = 464
+CALLS = ((0, 128), (128, 256), (256, 384), (384, 448), (448, 512))
+BIAS_ROW = 8
 
 
 def tile_picked_agg_lin_relu_sub_l_kernel(tc, xT, w_words, w_scales, b, gate, pos1, pos2, pos3, pos4, out):
@@ -41,13 +42,12 @@ def tile_picked_agg_lin_relu_sub_l_kernel(tc, xT, w_words, w_scales, b, gate, po
         lists = [keep.tile([P, V // 16], U16, align_bytes=ALIGN, name=f"list{d}") for d in range(D)]
         raw = [keep.tile([P, PACK, n], F32, align_bytes=ALIGN, name=f"raw{i}", tag=f"raw{i}") for i, (a, t0, n) in enumerate(LOADS)]
         whole = [keep.tile([P, T, PACK], BF16, align_bytes=ALIGN, name=f"whole{a}") for a in range(LAST)]
-        pieces = [keep.tile([P, GROUP, PACK], BF16, align_bytes=ALIGN, name=f"piece{g}") for g in range(GROUPS)]
+        pieces = {t0: keep.tile([P, t1 - t0, PACK], BF16, align_bytes=ALIGN, name=f"piece{t0}") for t0, t1 in CALLS}
 
         def rounded(a, t0, t1):
             if a < LAST:
                 return whole[a][:, t0:t1, :]
-            g = t0 // GROUP
-            return pieces[g][:, t0 - g * GROUP : t1 - g * GROUP, :]
+            return pieces[t0][:]
 
         codes = [keep.tile([P, T], U32, align_bytes=ALIGN, name=f"codes{a}") for a in range(PASSES)]
         scales = [keep.tile([P, T], U8, align_bytes=ALIGN, name=f"scales{a}") for a in range(PASSES)]
@@ -99,14 +99,14 @@ def tile_picked_agg_lin_relu_sub_l_kernel(tc, xT, w_words, w_scales, b, gate, po
                 in_=rounded(a, nodes.start, nodes.stop).rearrange("p c j -> p (c j)"),
             )
 
-        def multiply(sums, m, a, nodes):
+        def multiply(sums, m, a, nodes, first=0):
             nc.tensor.matmul_mx(
                 out=sums[:],
                 lhsT=w_codes[m][:, a, :].bitcast(FP8X4),
                 lhsT_scale=w_scale[:, a, m * P : (m + 1) * P],
                 rhs=codes[a][:, nodes].bitcast(FP8X4),
                 rhs_scale=scales[a][:, nodes],
-                start=(a == 0),
+                start=(a == first),
                 stop=(a == LAST),
             )
 
@@ -125,7 +125,7 @@ def tile_picked_agg_lin_relu_sub_l_kernel(tc, xT, w_words, w_scales, b, gate, po
 
         for queue, rows in ((nc.sync, slice(0, 2)), (nc.scalar, slice(2, 4))):
             queue.dma_start(out=raw[0][:, rows, :], in_=x_rows[0][:, rows, :])
-        nc.sync.dma_start(out=bias_rows[0:BLOCKS, :], in_=b.rearrange("(m p) o -> m (p o)", p=P))
+        nc.sync.dma_start(out=bias_rows[BIAS_ROW : BIAS_ROW + BLOCKS, :], in_=b.rearrange("(m p) o -> m (p o)", p=P))
         load_x(1)
         for q in range(P // QUADRANT):
             nc.sync.dma_start(
@@ -136,9 +136,9 @@ def tile_picked_agg_lin_relu_sub_l_kernel(tc, xT, w_words, w_scales, b, gate, po
         for i in range(LAST, len(LOADS)):
             load_x(i)
         load_w(0, LAST, PASSES)
+        load_w(1, 0, LAST)
         load_list(0)
         load_gates(0, 1)
-        load_w(1, 0, LAST)
         load_list(1)
         load_gates(1, 3)
         load_w(1, LAST, PASSES)
@@ -147,31 +147,31 @@ def tile_picked_agg_lin_relu_sub_l_kernel(tc, xT, w_words, w_scales, b, gate, po
         load_list(3)
 
         nc.tensor.transpose(bias_psum[:], bias_rows[:], identity[:])
-        nc.vector.tensor_copy(out=bias[:], in_=bias_psum[:, 0:BLOCKS])
+        nc.vector.tensor_copy(out=bias[:], in_=bias_psum[:, BIAS_ROW : BIAS_ROW + BLOCKS])
 
         by_vector, by_scalar = nc.vector.tensor_copy, nc.scalar.copy
         groups = [slice(g * GROUP, (g + 1) * GROUP) for g in range(GROUPS)]
 
-        def block0_pass(a):
-            for g in range(GROUPS):
-                quantize(a, groups[g])
-                multiply(sums0[g], 0, a, groups[g])
-
         interleave(by_vector, 0, 0, T)
         quantize(0, slice(0, T))
-        for g in range(GROUPS):
-            multiply(sums0[g], 0, 0, groups[g])
         interleave(by_vector, 1, 0, GROUP)
         interleave(by_vector, 1, GROUP, 2 * GROUP)
         interleave(by_scalar, 1, 2 * GROUP, 3 * GROUP)
         interleave(by_scalar, 1, 3 * GROUP, T)
-        block0_pass(1)
+        for g in range(GROUPS):
+            quantize(1, groups[g])
+            multiply(sums0[g], 0, 1, groups[g], first=1)
+            multiply(sums0[g], 0, 0, groups[g], first=1)
         interleave(by_vector, LAST, 0, GROUP)
         interleave(by_scalar, LAST, GROUP, 2 * GROUP)
         interleave(by_scalar, LAST + 1, 2 * GROUP, 3 * GROUP)
-        interleave(by_vector, LAST + 2, 3 * GROUP, END_SPLIT)
-        interleave(by_scalar, LAST + 2, END_SPLIT, T)
-        block0_pass(LAST)
+        interleave(by_vector, LAST + 2, *CALLS[3])
+        interleave(by_scalar, LAST + 2, *CALLS[4])
+        for t0, t1 in CALLS:
+            quantize(LAST, slice(t0, t1))
+            if t1 % GROUP == 0:
+                g = t1 // GROUP - 1
+                multiply(sums0[g], 0, LAST, groups[g], first=1)
         for g in range(GROUPS):
             finish(sums0[g], 0, groups[g])
 

@@ -117,7 +117,10 @@ def tile_picked_agg_lin_relu_sub_l_kernel(tc, xT, w_words, w_scales, b, gate, po
             return gates[:, 1, :] if (m, d) == (0, D - 1) else products[m][:, d, :]
 
         def gather(m, d):
-            nc.vector.tensor_tensor(product(m, d), y[m][:].indirect(lists[d][:]), gates[:, d, :], MULT)
+            parts = HALVES if m == 1 and d >= D - 2 else 1
+            for i in range(parts):
+                c0, c1 = i * V // parts, (i + 1) * V // parts
+                nc.vector.tensor_tensor(product(m, d)[:, c0:c1], y[m][:].indirect(lists[d][:, c0 // 16 : c1 // 16]), gates[:, d, c0:c1], MULT)
 
         nc.vector.memset(w_scale[:].rearrange("p a n -> p (a n)").bitcast(I32), 0)
         nc.vector.memset(bias_rows[:], 0.0)

@@ -29,7 +29,7 @@ QUADRANT = 32
 ALIGN = 256
 
 LOADS = ((0, 0, 512), (1, 0, 512), (2, 0, 256), (2, 256, 128), (2, 384, 128))
-CALLS = ((0, 128), (128, 256), (256, 384), (384, 448), (448, 512))
+CALLS = ((0, 128), (128, 256), (256, 384), (384, 448), (448, 480), (480, 512))
 BIAS_ROW = 8
 
 
@@ -169,7 +169,8 @@ def tile_picked_agg_lin_relu_sub_l_kernel(tc, xT, w_words, w_scales, b, gate, po
         interleave(by_scalar, LAST, GROUP, 2 * GROUP)
         interleave(by_scalar, LAST + 1, 2 * GROUP, 3 * GROUP)
         interleave(by_vector, LAST + 2, *CALLS[3])
-        interleave(by_scalar, LAST + 2, *CALLS[4])
+        for call in CALLS[4:]:
+            interleave(by_scalar, LAST + 2, *call)
         for t0, t1 in CALLS:
             quantize(LAST, slice(t0, t1))
             if t1 % GROUP == 0:

@@ -59,7 +59,10 @@ def tile_picked_agg_lin_relu_sub_l_kernel(tc, xT, w_words, w_scales, b, gate, po
         gates = keep.tile([P, D, V], F32, align_bytes=ALIGN, name="gates")
         y = [keep.tile([P, T], F32, align_bytes=ALIGN, name="y0", tag=f"raw{len(LOADS) - 1}"), keep.tile([P, T], F32, align_bytes=ALIGN, name="y1")]
         products = [keep.tile([P, D, V], F32, align_bytes=ALIGN, name=f"products{m}") for m in range(BLOCKS)]
-        turned_sb = [[keep.tile([P, P], F32, align_bytes=ALIGN, name=f"turned_sb{m}_{h}") for h in range(HALVES)] for m in range(BLOCKS)]
+        turned_sb = [
+            [products[1][:, 1, h * P : (h + 1) * P] for h in range(HALVES)],
+            [keep.tile([P, P], F32, align_bytes=ALIGN, name=f"turned_sb{h}") for h in range(HALVES)],
+        ]
         result = [keep.tile([P, V], F32, align_bytes=ALIGN, name=f"result{m}") for m in range(BLOCKS)]
 
         def bank(number, columns, name):
@@ -202,6 +205,7 @@ def tile_picked_agg_lin_relu_sub_l_kernel(tc, xT, w_words, w_scales, b, gate, po
                         start=(d == 0),
                         stop=(d == D - 2),
                     )
+        for m in range(BLOCKS):
             for h in range(HALVES):
                 nc.scalar.copy(out=turned_sb[m][h][:], in_=turned[m][h][:])
                 nc.tensor.transpose(back[m][h], turned_sb[m][h][:], identity[:])

@@ -120,7 +120,7 @@ def tile_picked_agg_lin_relu_sub_l_kernel(tc, xT, w_words, w_scales, b, gate, po
             return gates[:, 1, :] if (m, d) == (0, D - 1) else products[m][:, d, :]
 
         def gather(m, d):
-            parts = HALVES if m == 1 and d >= D - 2 else 1
+            parts = HALVES if (m, d) == (1, D - 2) else 1
             for i in range(parts):
                 c0, c1 = i * V // parts, (i + 1) * V // parts
                 nc.vector.tensor_tensor(product(m, d)[:, c0:c1], y[m][:].indirect(lists[d][:, c0 // 16 : c1 // 16]), gates[:, d, c0:c1], MULT)

@@ -29,7 +29,7 @@ QUADRANT = 32
 ALIGN = 256
 
 LOADS = ((0, 0, 512), (1, 0, 512), (2, 0, 256), (2, 256, 128), (2, 384, 128))
-CALLS = ((0, 128), (128, 256), (256, 384), (384, 448), (448, 480), (480, 512))
+CALLS = ((0, 128), (128, 256), (256, 384), (384, 448), (448, 512))
 BIAS_ROW = 8
 
 

@@ -59,10 +59,7 @@ def tile_picked_agg_lin_relu_sub_l_kernel(tc, xT, w_words, w_scales, b, gate, po
         gates = keep.tile([P, D, V], F32, align_bytes=ALIGN, name="gates")
         y = [keep.tile([P, T], F32, align_bytes=ALIGN, name="y0", tag=f"raw{len(LOADS) - 1}"), keep.tile([P, T], F32, align_bytes=ALIGN, name="y1")]
         products = [keep.tile([P, D, V], F32, align_bytes=ALIGN, name=f"products{m}") for m in range(BLOCKS)]
-        turned_sb = [
-            [products[1][:, 1, h * P : (h + 1) * P] for h in range(HALVES)],
-            [keep.tile([P, P], F32, align_bytes=ALIGN, name=f"turned_sb{h}") for h in range(HALVES)],
-        ]
+        turned_sb = [[keep.tile([P, P], F32, align_bytes=ALIGN, name=f"turned_sb{m}_{h}") for h in range(HALVES)] for m in range(BLOCKS)]
         result = [keep.tile([P, V], F32, align_bytes=ALIGN, name=f"result{m}") for m in range(BLOCKS)]
 
         def bank(number, columns, name):

@@ -30,7 +30,7 @@ ALIGN = 256
 
 LOADS = ((0, 0, 512), (1, 0, 512), (2, 0, 256), (2, 256, 128), (2, 384, 128))
 CALLS = ((0, 128), (128, 256), (256, 384), (384, 448), (448, 512))
-BIAS_ROW = 8
+BIAS_ROW = 0
 
 
 def tile_picked_agg_lin_relu_sub_l_kernel(tc, xT, w_words, w_scales, b, gate, pos1, pos2, pos3, pos4, out):
@@ -139,9 +139,9 @@ def tile_picked_agg_lin_relu_sub_l_kernel(tc, xT, w_words, w_scales, b, gate, po
         for i in range(LAST, len(LOADS)):
             load_x(i)
         load_w(0, LAST, PASSES)
-        load_w(1, 0, LAST)
         load_list(0)
         load_gates(0, 1)
+        load_w(1, 0, LAST)
         load_list(1)
         load_gates(1, 3)
         load_w(1, LAST, PASSES)

@@ -50,7 +50,7 @@ def tile_picked_agg_lin_relu_sub_l_kernel(tc, xT, w_words, w_scales, b, gate, po
             return pieces[t0][:]
 
         codes = [keep.tile([P, T], U32, align_bytes=ALIGN, name=f"codes{a}") for a in range(PASSES)]
-        scales = [keep.tile([P, T], U8, align_bytes=ALIGN, name=f"scales{a}") for a in range(PASSES)]
+        scales = [keep.tile([P, T + 128], U8, align_bytes=ALIGN, name=f"scales{a}")[:, 128:] for a in range(PASSES)]
         w_codes = [keep.tile([P, PASSES, P * PACK], U8, align_bytes=ALIGN, name=f"w_codes{m}") for m in range(BLOCKS)]
         w_scale = keep.tile([P, PASSES, N], U8, align_bytes=ALIGN, name="w_scale")
         identity = keep.tile([P, P], F32, align_bytes=ALIGN, name="identity")

@@ -13,7 +13,7 @@ U32 = mybir.dt.uint32
 U16 = mybir.dt.uint16
 U8 = mybir.dt.uint8
 FP8X4 = mybir.dt.float8_e4m3fn_x4
-RELU = mybir.ActivationFunctionType.Relu
+RELU, COPY = mybir.ActivationFunctionType.Relu, mybir.ActivationFunctionType.Copy
 ADD, MULT = mybir.AluOpType.add, mybir.AluOpType.mult
 
 P = 128
@@ -30,6 +30,8 @@ ALIGN = 256
 
 LOADS = ((0, 0, 512), (1, 0, 512), (2, 0, 256), (2, 256, 128), (2, 384, 128))
 CALLS = ((0, 128), (128, 256), (256, 384), (384, 448), (448, 512))
+ON_SCALAR = ((0, 2), (1, 2), (1, 3), (0, 3))
+SHARE = 128
 BIAS_ROW = 0
 
 
@@ -58,8 +60,11 @@ def tile_picked_agg_lin_relu_sub_l_kernel(tc, xT, w_words, w_scales, b, gate, po
         bias = keep.tile([P, BLOCKS], F32, align_bytes=ALIGN, name="bias")
         gates = keep.tile([P, D, V], F32, align_bytes=ALIGN, name="gates")
         y = [keep.tile([P, T], F32, align_bytes=ALIGN, name="y0", tag=f"raw{len(LOADS) - 1}"), keep.tile([P, T], F32, align_bytes=ALIGN, name="y1")]
-        products = [keep.tile([P, D, V], F32, align_bytes=ALIGN, name=f"products{m}") for m in range(BLOCKS)]
-        turned_sb = [[keep.tile([P, P], F32, align_bytes=ALIGN, name=f"turned_sb{m}_{h}") for h in range(HALVES)] for m in range(BLOCKS)]
+        products = {(m, d): keep.tile([P, V], F32, align_bytes=ALIGN, name=f"product{m}_{d}") for m in range(BLOCKS) for d in range(D) if (m, d) != (1, 0)}
+        pair = keep.tile([P, V], F32, align_bytes=ALIGN, name="pair")
+        turned_sb = [keep.tile([P, V], F32, align_bytes=ALIGN, name=f"turned_sb{m}") for m in range(BLOCKS)]
+        fetched = {(m, d): keep.tile([P, V], F32, align_bytes=ALIGN, name=f"fetched{m}_{d}") for m, d in ON_SCALAR}
+        products[1, 0] = fetched[0, 2]
         result = [keep.tile([P, V], F32, align_bytes=ALIGN, name=f"result{m}") for m in range(BLOCKS)]
 
         def bank(number, columns, name):
@@ -113,14 +118,14 @@ def tile_picked_agg_lin_relu_sub_l_kernel(tc, xT, w_words, w_scales, b, gate, po
         def finish(sums, m, nodes):
             nc.scalar.activation(out=y[m][:, nodes], in_=sums[:], func=RELU, bias=bias[:, m : m + 1], scale=1.0)
 
-        def product(m, d):
-            return gates[:, 1, :] if (m, d) == (0, D - 1) else products[m][:, d, :]
+        def gather(m, d, c0=0, c1=V):
+            nc.vector.tensor_tensor(products[m, d][:, c0:c1], y[m][:].indirect(lists[d][:, c0 // 16 : c1 // 16]), gates[:, d, c0:c1], MULT)
 
-        def gather(m, d):
-            parts = HALVES if (m, d) == (1, D - 2) else 1
-            for i in range(parts):
-                c0, c1 = i * V // parts, (i + 1) * V // parts
-                nc.vector.tensor_tensor(product(m, d)[:, c0:c1], y[m][:].indirect(lists[d][:, c0 // 16 : c1 // 16]), gates[:, d, c0:c1], MULT)
+        def fetch(m, d, c0=0, c1=V):
+            nc.scalar.activation(out=fetched[m, d][:, c0:c1], in_=y[m][:].indirect(lists[d][:, c0 // 16 : c1 // 16]), func=COPY)
+
+        def weigh(m, d, c0=0, c1=V):
+            nc.vector.tensor_tensor(products[m, d][:, c0:c1], fetched[m, d][:, c0:c1], gates[:, d, c0:c1], MULT)
 
         nc.vector.memset(w_scale[:].rearrange("p a n -> p (a n)").bitcast(I32), 0)
         nc.vector.memset(bias_rows[:], 0.0)
@@ -139,15 +144,15 @@ def tile_picked_agg_lin_relu_sub_l_kernel(tc, xT, w_words, w_scales, b, gate, po
         for i in range(LAST, len(LOADS)):
             load_x(i)
         load_w(0, LAST, PASSES)
+        load_w(1, 0, PASSES)
         load_list(0)
         load_gates(0, 1)
-        load_w(1, 0, LAST)
         load_list(1)
-        load_gates(1, 3)
-        load_w(1, LAST, PASSES)
+        load_gates(1, 2)
         load_list(2)
-        load_gates(3, 4)
         load_list(3)
+        load_gates(2, 3)
+        load_gates(3, 4)
 
         nc.tensor.transpose(bias_psum[:], bias_rows[:], identity[:])
         nc.vector.tensor_copy(out=bias[:], in_=bias_psum[:, BIAS_ROW : BIAS_ROW + BLOCKS])
@@ -171,6 +176,7 @@ def tile_picked_agg_lin_relu_sub_l_kernel(tc, xT, w_words, w_scales, b, gate, po
         interleave(by_vector, LAST + 2, *CALLS[3])
         for call in CALLS[4:]:
             interleave(by_scalar, LAST + 2, *call)
+        node_halves = [slice(h * T // 2, (h + 1) * T // 2) for h in range(2)]
         for t0, t1 in CALLS:
             quantize(LAST, slice(t0, t1))
             if t1 % GROUP == 0:
@@ -178,39 +184,47 @@ def tile_picked_agg_lin_relu_sub_l_kernel(tc, xT, w_words, w_scales, b, gate, po
                 multiply(sums0[g], 0, LAST, groups[g], first=1)
         for g in range(GROUPS):
             finish(sums0[g], 0, groups[g])
-
-        node_halves = [slice(h * T // 2, (h + 1) * T // 2) for h in range(2)]
-        for a in range(PASSES):
-            for h in range(2):
-                multiply(sums1[h], 1, a, node_halves[h])
         for h in range(2):
-            finish(sums1[h], 1, node_halves[h])
+            for a in range(PASSES):
+                multiply(sums1[h], 1, a, node_halves[h])
 
-        turned = [[bank(GROUPS + HALVES * m + h, P, f"turned{m}_{h}") for h in range(HALVES)] for m in range(BLOCKS)]
         targets = [slice(h * P, (h + 1) * P) for h in range(HALVES)]
+        turned = [[bank(GROUPS + HALVES * m + h, P, f"turned{m}_{h}") for h in range(HALVES)] for m in range(BLOCKS)]
         back0 = bank(0, V, "back0")
         back = [[back0[:, half] for half in targets], [bank(1 + h, P, f"back1_{h}")[:] for h in range(HALVES)]]
+
+        def turn(m, d):
+            for h in range(HALVES):
+                nc.tensor.matmul(
+                    turned[m][h][:], lhsT=products[m, d][:, targets[h]], rhs=identity[:], is_transpose=True, start=(d == m), stop=(d == 2)
+                )
+
+        def add(total, one, other):
+            nc.vector.tensor_tensor(total, one, other, ADD)
+
+        for h in range(2):
+            finish(sums1[h], 1, node_halves[h])
+        for m, d in ON_SCALAR[:-1]:
+            fetch(m, d)
+        fetch(0, 3, 0, SHARE)
+        for m, d in ((0, 0), (0, 1), (1, 1)):
+            gather(m, d)
+            turn(m, d)
         for m in range(BLOCKS):
-            for d in range(D - 1):
-                gather(m, d)
-                for h in range(HALVES):
-                    nc.tensor.matmul(
-                        turned[m][h][:],
-                        lhsT=products[m][:, d, targets[h]],
-                        rhs=identity[:],
-                        is_transpose=True,
-                        start=(d == 0),
-                        stop=(d == D - 2),
-                    )
+            weigh(m, 2)
+            turn(m, 2)
+        gather(1, 0)
+        weigh(1, 3)
+        gather(0, 3, SHARE, V)
+        weigh(0, 3, 0, SHARE)
         for m in range(BLOCKS):
             for h in range(HALVES):
-                nc.scalar.copy(out=turned_sb[m][h][:], in_=turned[m][h][:])
-                nc.tensor.transpose(back[m][h], turned_sb[m][h][:], identity[:])
+                nc.scalar.copy(out=turned_sb[m][:, targets[h]], in_=turned[m][h][:])
+                nc.tensor.transpose(back[m][h], turned_sb[m][:, targets[h]], identity[:])
 
-        for m in range(BLOCKS):
-            gather(m, D - 1)
-        nc.vector.tensor_tensor(result[0][:], product(0, D - 1), back0[:], ADD)
+        add(pair[:], products[1, 0][:], products[1, 3][:])
+        add(result[0][:], products[0, 3][:], back0[:])
         nc.sync.dma_start(out=out[0:P, :], in_=result[0][:])
         for h in range(HALVES):
-            nc.vector.tensor_tensor(result[1][:, targets[h]], product(1, D - 1)[:, targets[h]], back[1][h], ADD)
+            add(result[1][:, targets[h]], pair[:, targets[h]], back[1][h])
         nc.sync.dma_start(out=out[P:N, :], in_=result[1][:])

@@ -147,9 +147,9 @@ def tile_picked_agg_lin_relu_sub_l_kernel(tc, xT, w_words, w_scales, b, gate, po
         load_w(1, 0, PASSES)
         load_list(0)
         load_gates(0, 1)
+        load_list(2)
         load_list(1)
         load_gates(1, 2)
-        load_list(2)
         load_list(3)
         load_gates(2, 3)
         load_gates(3, 4)

@@ -31,7 +31,6 @@ ALIGN = 256
 LOADS = ((0, 0, 512), (1, 0, 512), (2, 0, 256), (2, 256, 128), (2, 384, 128))
 CALLS = ((0, 128), (128, 256), (256, 384), (384, 448), (448, 512))
 ON_SCALAR = ((0, 2), (1, 2), (1, 3), (0, 3))
-SHARE = 128
 BIAS_ROW = 0
 
 
@@ -71,8 +70,10 @@ def tile_picked_agg_lin_relu_sub_l_kernel(tc, xT, w_words, w_scales, b, gate, po
             return psum.tile([P, columns], F32, name=name, tag=f"bank{number}")
 
         bias_psum = bank(7, P, "bias_psum")
-        sums0 = [bank(g, GROUP, f"sums0_{g}") for g in range(GROUPS)]
-        sums1 = [bank(GROUPS + h, T // 2, f"sums1_{h}") for h in range(2)]
+        shared = bank(GROUPS - 1, 2 * GROUP, "shared")
+        sums0 = [bank(g, GROUP, f"sums0_{g}")[:] for g in range(GROUPS - 1)] + [shared[:, :GROUP]]
+        sums1 = [shared[:, GROUP:], bank(GROUPS, 2 * GROUP, "sums1_1")[:], bank(GROUPS + 1, GROUP, "sums1_2")[:]]
+        parts = [slice(0, GROUP), slice(GROUP, 3 * GROUP), slice(3 * GROUP, T)]
 
         x_rows = xT.rearrange("(a p j) t -> a p j t", p=P, j=PACK)
 
@@ -104,19 +105,19 @@ def tile_picked_agg_lin_relu_sub_l_kernel(tc, xT, w_words, w_scales, b, gate, po
                 in_=rounded(a, nodes.start, nodes.stop).rearrange("p c j -> p (c j)"),
             )
 
-        def multiply(sums, m, a, nodes, first=0):
+        def multiply(sums, m, a, nodes, start=False, stop=False):
             nc.tensor.matmul_mx(
-                out=sums[:],
+                out=sums,
                 lhsT=w_codes[m][:, a, :].bitcast(FP8X4),
                 lhsT_scale=w_scale[:, a, m * P : (m + 1) * P],
                 rhs=codes[a][:, nodes].bitcast(FP8X4),
                 rhs_scale=scales[a][:, nodes],
-                start=(a == first),
-                stop=(a == LAST),
+                start=start,
+                stop=stop,
             )
 
         def finish(sums, m, nodes):
-            nc.scalar.activation(out=y[m][:, nodes], in_=sums[:], func=RELU, bias=bias[:, m : m + 1], scale=1.0)
+            nc.scalar.activation(out=y[m][:, nodes], in_=sums, func=RELU, bias=bias[:, m : m + 1], scale=1.0)
 
         def gather(m, d, c0=0, c1=V):
             nc.vector.tensor_tensor(products[m, d][:, c0:c1], y[m][:].indirect(lists[d][:, c0 // 16 : c1 // 16]), gates[:, d, c0:c1], MULT)
@@ -168,25 +169,27 @@ def tile_picked_agg_lin_relu_sub_l_kernel(tc, xT, w_words, w_scales, b, gate, po
         interleave(by_scalar, 1, 3 * GROUP, T)
         for g in range(GROUPS):
             quantize(1, groups[g])
-            multiply(sums0[g], 0, 1, groups[g], first=1)
-            multiply(sums0[g], 0, 0, groups[g], first=1)
+            multiply(sums0[g], 0, 1, groups[g], start=True)
+            multiply(sums0[g], 0, 0, groups[g])
         interleave(by_vector, LAST, 0, GROUP)
         interleave(by_scalar, LAST, GROUP, 2 * GROUP)
         interleave(by_scalar, LAST + 1, 2 * GROUP, 3 * GROUP)
         interleave(by_vector, LAST + 2, *CALLS[3])
         for call in CALLS[4:]:
             interleave(by_scalar, LAST + 2, *call)
-        node_halves = [slice(h * T // 2, (h + 1) * T // 2) for h in range(2)]
         for t0, t1 in CALLS:
             quantize(LAST, slice(t0, t1))
             if t1 % GROUP == 0:
                 g = t1 // GROUP - 1
-                multiply(sums0[g], 0, LAST, groups[g], first=1)
+                if g == GROUPS - 1:
+                    for a in range(PASSES):
+                        multiply(sums1[0], 1, a, parts[0])
+                multiply(sums0[g], 0, LAST, groups[g], stop=True)
         for g in range(GROUPS):
             finish(sums0[g], 0, groups[g])
-        for h in range(2):
+        for i in range(1, len(parts)):
             for a in range(PASSES):
-                multiply(sums1[h], 1, a, node_halves[h])
+                multiply(sums1[i], 1, a, parts[i], start=(a == 0), stop=(a == LAST))
 
         targets = [slice(h * P, (h + 1) * P) for h in range(HALVES)]
         turned = [[bank(GROUPS + HALVES * m + h, P, f"turned{m}_{h}") for h in range(HALVES)] for m in range(BLOCKS)]
@@ -202,11 +205,10 @@ def tile_picked_agg_lin_relu_sub_l_kernel(tc, xT, w_words, w_scales, b, gate, po
         def add(total, one, other):
             nc.vector.tensor_tensor(total, one, other, ADD)
 
-        for h in range(2):
-            finish(sums1[h], 1, node_halves[h])
-        for m, d in ON_SCALAR[:-1]:
+        for i in range(len(parts)):
+            finish(sums1[i], 1, parts[i])
+        for m, d in ON_SCALAR:
             fetch(m, d)
-        fetch(0, 3, 0, SHARE)
         for m, d in ((0, 0), (0, 1), (1, 1)):
             gather(m, d)
             turn(m, d)
@@ -215,8 +217,7 @@ def tile_picked_agg_lin_relu_sub_l_kernel(tc, xT, w_words, w_scales, b, gate, po
             turn(m, 2)
         gather(1, 0)
         weigh(1, 3)
-        gather(0, 3, SHARE, V)
-        weigh(0, 3, 0, SHARE)
+        weigh(0, 3)
         for m in range(BLOCKS):
             for h in range(HALVES):
                 nc.scalar.copy(out=turned_sb[m][:, targets[h]], in_=turned[m][h][:])

@@ -193,14 +193,10 @@ def tile_picked_agg_lin_relu_sub_l_kernel(tc, xT, w_words, w_scales, b, gate, po
 
         targets = [slice(h * P, (h + 1) * P) for h in range(HALVES)]
         turned = [[bank(GROUPS + HALVES * m + h, P, f"turned{m}_{h}") for h in range(HALVES)] for m in range(BLOCKS)]
-        back0 = bank(0, V, "back0")
-        back = [[back0[:, half] for half in targets], [bank(1 + h, P, f"back1_{h}")[:] for h in range(HALVES)]]
+        back = [[bank(HALVES * m + h, P, f"back{m}_{h}")[:] for h in range(HALVES)] for m in range(BLOCKS)]
 
-        def turn(m, d):
-            for h in range(HALVES):
-                nc.tensor.matmul(
-                    turned[m][h][:], lhsT=products[m, d][:, targets[h]], rhs=identity[:], is_transpose=True, start=(d == m), stop=(d == 2)
-                )
+        def turn(m, d, h):
+            nc.tensor.matmul(turned[m][h][:], lhsT=products[m, d][:, targets[h]], rhs=identity[:], is_transpose=True, start=(d == m), stop=(d == 2))
 
         def add(total, one, other):
             nc.vector.tensor_tensor(total, one, other, ADD)
@@ -211,10 +207,14 @@ def tile_picked_agg_lin_relu_sub_l_kernel(tc, xT, w_words, w_scales, b, gate, po
             fetch(m, d)
         for m, d in ((0, 0), (0, 1), (1, 1)):
             gather(m, d)
-            turn(m, d)
-        for m in range(BLOCKS):
-            weigh(m, 2)
-            turn(m, 2)
+            for h in range(HALVES):
+                turn(m, d, h)
+        weigh(0, 2)
+        for h in range(HALVES):
+            turn(0, 2, h)
+        for h in range(HALVES):
+            weigh(1, 2, h * P, (h + 1) * P)
+            turn(1, 2, h)
         gather(1, 0)
         weigh(1, 3)
         weigh(0, 3)
@@ -224,7 +224,8 @@ def tile_picked_agg_lin_relu_sub_l_kernel(tc, xT, w_words, w_scales, b, gate, po
                 nc.tensor.transpose(back[m][h], turned_sb[m][:, targets[h]], identity[:])
 
         add(pair[:], products[1, 0][:], products[1, 3][:])
-        add(result[0][:], products[0, 3][:], back0[:])
+        for h in range(HALVES):
+            add(result[0][:, targets[h]], products[0, 3][:, targets[h]], back[0][h])
         nc.sync.dma_start(out=out[0:P, :], in_=result[0][:])
         for h in range(HALVES):
             add(result[1][:, targets[h]], pair[:, targets[h]], back[1][h])

from contextlib import ExitStack

import concourse.mybir as mybir
from concourse.masks import make_identity

K, T, D, V, N = 1536, 512, 4, 256, 256
FLOPS = 2 * K * T * N

F32 = mybir.dt.float32
BF16 = mybir.dt.bfloat16
I32 = mybir.dt.int32
U32 = mybir.dt.uint32
U16 = mybir.dt.uint16
U8 = mybir.dt.uint8
FP8X4 = mybir.dt.float8_e4m3fn_x4
RELU, COPY = mybir.ActivationFunctionType.Relu, mybir.ActivationFunctionType.Copy
ADD, MULT = mybir.AluOpType.add, mybir.AluOpType.mult

P = 128
PACK = 4
PASSES = K // (P * PACK)
LAST = PASSES - 1
BLOCKS = N // P
GROUP = 128
GROUPS = T // GROUP
HALVES = V // P
RUN = 4
QUADRANT = 32
ALIGN = 256

LOADS = ((0, 0, 512), (1, 0, 512), (2, 0, 256), (2, 256, 128), (2, 384, 128))
CALLS = ((0, 128), (128, 256), (256, 384), (384, 448), (448, 512))
ON_SCALAR = ((0, 2), (1, 2), (1, 3), (0, 3))
BIAS_ROW = 0


def tile_picked_agg_lin_relu_sub_l_kernel(tc, xT, w_words, w_scales, b, gate, pos1, pos2, pos3, pos4, out):
    nc = tc.nc
    with ExitStack() as ctx:
        keep = ctx.enter_context(tc.tile_pool(name="keep", bufs=1))
        psum = ctx.enter_context(tc.psum_pool(name="psum", bufs=1))

        lists = [keep.tile([P, V // 16], U16, align_bytes=ALIGN, name=f"list{d}") for d in range(D)]
        raw = [keep.tile([P, PACK, n], F32, align_bytes=ALIGN, name=f"raw{i}", tag=f"raw{i}") for i, (a, t0, n) in enumerate(LOADS)]
        whole = [keep.tile([P, T, PACK], BF16, align_bytes=ALIGN, name=f"whole{a}") for a in range(LAST)]
        pieces = {t0: keep.tile([P, t1 - t0, PACK], BF16, align_bytes=ALIGN, name=f"piece{t0}") for t0, t1 in CALLS}

        def rounded(a, t0, t1):
            if a < LAST:
                return whole[a][:, t0:t1, :]
            return pieces[t0][:]

        codes = [keep.tile([P, T], U32, align_bytes=ALIGN, name=f"codes{a}") for a in range(PASSES)]
        scales = [keep.tile([P, T + 128], U8, align_bytes=ALIGN, name=f"scales{a}")[:, 128:] for a in range(PASSES)]
        w_codes = [keep.tile([P, PASSES, P * PACK], U8, align_bytes=ALIGN, name=f"w_codes{m}") for m in range(BLOCKS)]
        w_scale = keep.tile([P, PASSES, N], U8, align_bytes=ALIGN, name="w_scale")
        identity = keep.tile([P, P], F32, align_bytes=ALIGN, name="identity")
        bias_rows = keep.tile([P, P], F32, align_bytes=ALIGN, name="bias_rows")
        bias = keep.tile([P, BLOCKS], F32, align_bytes=ALIGN, name="bias")
        gates = keep.tile([P, D, V], F32, align_bytes=ALIGN, name="gates")
        y = [keep.tile([P, T], F32, align_bytes=ALIGN, name="y0", tag=f"raw{len(LOADS) - 1}"), keep.tile([P, T], F32, align_bytes=ALIGN, name="y1")]
        products = {(m, d): keep.tile([P, V], F32, align_bytes=ALIGN, name=f"product{m}_{d}") for m in range(BLOCKS) for d in range(D) if (m, d) != (1, 0)}
        pair = keep.tile([P, V], F32, align_bytes=ALIGN, name="pair")
        turned_sb = [keep.tile([P, V], F32, align_bytes=ALIGN, name=f"turned_sb{m}") for m in range(BLOCKS)]
        fetched = {(m, d): keep.tile([P, V], F32, align_bytes=ALIGN, name=f"fetched{m}_{d}") for m, d in ON_SCALAR}
        products[1, 0] = fetched[0, 2]
        result = [keep.tile([P, V], F32, align_bytes=ALIGN, name=f"result{m}") for m in range(BLOCKS)]

        def bank(number, columns, name):
            return psum.tile([P, columns], F32, name=name, tag=f"bank{number}")

        bias_psum = bank(7, P, "bias_psum")
        shared = bank(GROUPS - 1, 2 * GROUP, "shared")
        sums0 = [bank(g, GROUP, f"sums0_{g}")[:] for g in range(GROUPS - 1)] + [shared[:, :GROUP]]
        sums1 = [shared[:, GROUP:], bank(GROUPS, 2 * GROUP, "sums1_1")[:], bank(GROUPS + 1, GROUP, "sums1_2")[:]]
        parts = [slice(0, GROUP), slice(GROUP, 3 * GROUP), slice(3 * GROUP, T)]

        x_rows = xT.rearrange("(a p j) t -> a p j t", p=P, j=PACK)

        def load_x(i):
            a, t0, n = LOADS[i]
            nc.sync.dma_start(out=raw[i][:], in_=x_rows[a][:, :, t0 : t0 + n])

        def load_w(m, a0, a1):
            words = w_words[a0:a1, :, m * P : (m + 1) * P, :].rearrange("a p n r -> p a (n r)")
            nc.sync.dma_start(out=w_codes[m][:, a0:a1, :], in_=words)

        def load_list(d):
            nc.sync.dma_start(lists[d][:], (pos1, pos2, pos3, pos4)[d])

        def load_gates(d0, d1):
            nc.sync.dma_start(out=gates[:, d0:d1, :], in_=gate[d0:d1, 0:P, :].rearrange("d p v -> p d v"))

        def interleave(copy, i, t0, t1):
            a, first, n = LOADS[i]
            copy(
                out=rounded(a, t0, t1).rearrange("p (c s) j -> p c j s", s=RUN),
                in_=raw[i][:, :, t0 - first : t1 - first].rearrange("p j (c s) -> p c j s", s=RUN),
            )

        def quantize(a, nodes):
            nc.vector.quantize_mx(
                out=codes[a][:, nodes].bitcast(FP8X4),
                scales=scales[a][:, nodes],
                in_=rounded(a, nodes.start, nodes.stop).rearrange("p c j -> p (c j)"),
            )

        def multiply(sums, m, a, nodes, start=False, stop=False):
            nc.tensor.matmul_mx(
                out=sums,
                lhsT=w_codes[m][:, a, :].bitcast(FP8X4),
                lhsT_scale=w_scale[:, a, m * P : (m + 1) * P],
                rhs=codes[a][:, nodes].bitcast(FP8X4),
                rhs_scale=scales[a][:, nodes],
                start=start,
                stop=stop,
            )

        def finish(sums, m, nodes):
            nc.scalar.activation(out=y[m][:, nodes], in_=sums, func=RELU, bias=bias[:, m : m + 1], scale=1.0)

        def gather(m, d, c0=0, c1=V):
            nc.vector.tensor_tensor(products[m, d][:, c0:c1], y[m][:].indirect(lists[d][:, c0 // 16 : c1 // 16]), gates[:, d, c0:c1], MULT)

        def fetch(m, d, c0=0, c1=V):
            nc.scalar.activation(out=fetched[m, d][:, c0:c1], in_=y[m][:].indirect(lists[d][:, c0 // 16 : c1 // 16]), func=COPY)

        def weigh(m, d, c0=0, c1=V):
            nc.vector.tensor_tensor(products[m, d][:, c0:c1], fetched[m, d][:, c0:c1], gates[:, d, c0:c1], MULT)

        nc.vector.memset(w_scale[:].rearrange("p a n -> p (a n)").bitcast(I32), 0)
        nc.vector.memset(bias_rows[:], 0.0)
        make_identity(nc, identity[:])

        for queue, rows in ((nc.sync, slice(0, 2)), (nc.scalar, slice(2, 4))):
            queue.dma_start(out=raw[0][:, rows, :], in_=x_rows[0][:, rows, :])
        nc.sync.dma_start(out=bias_rows[BIAS_ROW : BIAS_ROW + BLOCKS, :], in_=b.rearrange("(m p) o -> m (p o)", p=P))
        load_x(1)
        for q in range(P // QUADRANT):
            nc.sync.dma_start(
                out=w_scale[QUADRANT * q : QUADRANT * q + 4, :, :].bitcast(I32),
                in_=w_scales[:, 4 * q : 4 * q + 4, :].rearrange("a r n -> r a n").bitcast(I32),
            )
        load_w(0, 0, LAST)
        for i in range(LAST, len(LOADS)):
            load_x(i)
        load_w(0, LAST, PASSES)
        load_w(1, 0, PASSES)
        load_list(0)
        load_gates(0, 1)
        load_list(2)
        load_list(1)
        load_gates(1, 2)
        load_list(3)
        load_gates(2, 3)
        load_gates(3, 4)

        nc.tensor.transpose(bias_psum[:], bias_rows[:], identity[:])
        nc.vector.tensor_copy(out=bias[:], in_=bias_psum[:, BIAS_ROW : BIAS_ROW + BLOCKS])

        by_vector, by_scalar = nc.vector.tensor_copy, nc.scalar.copy
        groups = [slice(g * GROUP, (g + 1) * GROUP) for g in range(GROUPS)]

        interleave(by_vector, 0, 0, T)
        quantize(0, slice(0, T))
        interleave(by_vector, 1, 0, GROUP)
        interleave(by_vector, 1, GROUP, 2 * GROUP)
        interleave(by_scalar, 1, 2 * GROUP, 3 * GROUP)
        interleave(by_scalar, 1, 3 * GROUP, T)
        for g in range(GROUPS):
            quantize(1, groups[g])
            multiply(sums0[g], 0, 1, groups[g], start=True)
            multiply(sums0[g], 0, 0, groups[g])
        interleave(by_vector, LAST, 0, GROUP)
        interleave(by_scalar, LAST, GROUP, 2 * GROUP)
        interleave(by_scalar, LAST + 1, 2 * GROUP, 3 * GROUP)
        interleave(by_vector, LAST + 2, *CALLS[3])
        for call in CALLS[4:]:
            interleave(by_scalar, LAST + 2, *call)
        for t0, t1 in CALLS:
            quantize(LAST, slice(t0, t1))
            if t1 % GROUP == 0:
                g = t1 // GROUP - 1
                if g == GROUPS - 1:
                    for a in range(PASSES):
                        multiply(sums1[0], 1, a, parts[0])
                multiply(sums0[g], 0, LAST, groups[g], stop=True)
        for g in range(GROUPS):
            finish(sums0[g], 0, groups[g])
        for i in range(1, len(parts)):
            for a in range(PASSES):
                multiply(sums1[i], 1, a, parts[i], start=(a == 0), stop=(a == LAST))

        targets = [slice(h * P, (h + 1) * P) for h in range(HALVES)]
        turned = [[bank(GROUPS + HALVES * m + h, P, f"turned{m}_{h}") for h in range(HALVES)] for m in range(BLOCKS)]
        back = [[bank(HALVES * m + h, P, f"back{m}_{h}")[:] for h in range(HALVES)] for m in range(BLOCKS)]

        def turn(m, d, h):
            nc.tensor.matmul(turned[m][h][:], lhsT=products[m, d][:, targets[h]], rhs=identity[:], is_transpose=True, start=(d == m), stop=(d == 2))

        def add(total, one, other):
            nc.vector.tensor_tensor(total, one, other, ADD)

        for i in range(len(parts)):
            finish(sums1[i], 1, parts[i])
        for m, d in ON_SCALAR:
            fetch(m, d)
        for m, d in ((0, 0), (0, 1), (1, 1)):
            gather(m, d)
            for h in range(HALVES):
                turn(m, d, h)
        weigh(0, 2)
        for h in range(HALVES):
            turn(0, 2, h)
        for h in range(HALVES):
            weigh(1, 2, h * P, (h + 1) * P)
            turn(1, 2, h)
        gather(1, 0)
        weigh(1, 3)
        weigh(0, 3)
        for m in range(BLOCKS):
            for h in range(HALVES):
                nc.scalar.copy(out=turned_sb[m][:, targets[h]], in_=turned[m][h][:])
                nc.tensor.transpose(back[m][h], turned_sb[m][:, targets[h]], identity[:])

        add(pair[:], products[1, 0][:], products[1, 3][:])
        for h in range(HALVES):
            add(result[0][:, targets[h]], products[0, 3][:, targets[h]], back[0][h])
        nc.sync.dma_start(out=out[0:P, :], in_=result[0][:])
        for h in range(HALVES):
            add(result[1][:, targets[h]], pair[:, targets[h]], back[1][h])
        nc.sync.dma_start(out=out[P:N, :], in_=result[1][:])
